import numpy as np, ml_dtypes
CORES = [40,41,42,43,44,45,46,47]
N = 8
import mx_ref
BF = ml_dtypes.bfloat16
def cut(t, i, w=512):
    return t[:, w * i:w * i + w]
def pick(q, e):
    c = np.concatenate([q[0].reshape(128, -1, 4), np.zeros((128, 1, 4), np.uint8)], axis=1); s = np.concatenate([q[1], np.ones((16, 1), np.uint8)], axis=1)
    return (np.ascontiguousarray(c[:, e].reshape(128, -1)), np.ascontiguousarray(s[:, e]))
def join(*qs):
    return (np.concatenate([q[0] for q in qs], axis=1), np.concatenate([q[1] for q in qs], axis=1))
def put(q, e, v):
    c, s = q[0].reshape(128, -1, 4).copy(), q[1].copy(); c[:, e] = v[0].reshape(128, -1, 4); s[:, e] = v[1]
    return (c.reshape(128, -1), s)
def pk(c, s):
    return (np.ascontiguousarray(c), mx_ref.live(s))
def emit(q):
    return q[0], q[1]
def decode(q):
    o = []
    for b in range(4):
        e = np.zeros((128, 128, 4), np.float32); e[np.arange(128), np.arange(128), b] = 1
        o.append(mx_ref.matmul(mx_ref.quantize(e.reshape(128, 512).astype(BF)), q))
    return np.stack(o, axis=2).reshape(128, -1)
def f(rng, *shape):
    return mx_ref.flush((rng.standard_normal(shape, dtype=np.float32) * np.exp2(rng.integers(-2, 3, shape[:-1] + (1,)))).astype(BF))
def wide(rng, *shape, cols=0):
    v = rng.standard_normal(shape, dtype=np.float32) * np.exp2(rng.integers(-12, 13, shape)).astype(np.float32)
    if cols: v *= np.repeat(np.exp2(rng.integers(-cols, cols + 1, shape[:-2] + (1, shape[-1] // 4))) * (rng.random(shape[:-2] + (1, shape[-1] // 4)) > 0.0625), 4, axis=-1).astype(np.float32)
    return mx_ref.flush(v.astype(BF))
P, K, O = 256, 64, 1
def places(t, j):
    return (j + t * np.arange(N)[:, None]) % P
def checks(tab, u):
    return np.stack([mx_ref.matmul(mx_ref.quantize(np.ascontiguousarray(u[r])), tab[r])[:2] for r in range(N)], axis=1)
def judge(c, g, t):
    j = np.arange(P)
    p = (j + t) % N
    at = places(t, j)
    c, a = c[np.arange(N)[:, None], at], np.abs(g[np.arange(N)[:, None], at])
    s = c[p, j]
    for r in range(N):
        s = np.where(p == r, s, s - c[r])
    bad = np.argsort(-np.abs(s), kind="stable")[:K]
    a[p, j] = -1
    return bad, np.argmax(a, axis=0)[bad]
def rebuilt(tab, bad, lost, t):
    at = places(t, bad)
    v = decode(join(*[pick(tab[r], at[r]) for r in range(N)])).reshape(128, N, K, 4)
    new = np.zeros((128, K, 4), np.float32)
    for k in range(K):
        p = (bad[k] + t) % N
        x = v[:, p, k]
        for r in range(N):
            if r != p and r != lost[k]: x = x - v[:, r, k]
        new[:, k] = x
    return mx_ref.quantize(np.ascontiguousarray(new.reshape(128, -1).astype(BF)))
def data(rng):
    return f(rng, N, 128, 4 * P).astype(np.float32).reshape(N, 128, P, 4)
def striped(v):
    v = v.copy()
    for r in range(N):
        j = np.arange(r, P, N)
        v[r][:, j] = 0
        v[r][:, j] = np.sum(v[:, :, j], axis=0)
    return v
def harm(rng, v, stripes, size):
    for j in stripes:
        v[(j + rng.integers(1, N)) % N][:, j] = size * rng.standard_normal((128, 4))
def queries(rng):
    q = np.array(f(rng, 1, 128, 512))
    q[:, :, 8:] = 0
    return np.concatenate([q] * N)
def draw(rng, v, q=None):
    v = v.astype(np.float32).reshape(N, 128, 4 * P)
    v[np.abs(v) < np.float32(2.0 ** -16)] = 0
    return {"tb": v.astype(BF), "u": queries(rng) if q is None else q, "w": f(rng, N, 128, 512 * O)}
def setup_inputs(rng):
    v = striped(data(rng))
    harm(rng, v, rng.permutation(P)[:K + 6], 8)
    return draw(rng, v)
def setup_inputs_again(rng):
    v, q = striped(data(rng) * np.float32(2.0 ** -8)), queries(rng)
    s = np.where(q[0, :, 4:8].astype(np.float32) < 0, -1.0, 1.0)
    q[:, :, :4] = (np.abs(q[:, :, :4].astype(np.float32)) * s).astype(BF)
    q[:, :32, :4] = 0
    on = (np.arange(128) < 32)[:, None]
    at = N * rng.permutation(P // N)[:K // 2] + 2 * rng.integers(0, N // 2, K // 2) + np.arange(K // 2) % 2
    for j in at:
        p = int(j) % N
        m = (p + int(rng.integers(1, N))) % N
        if p % 2:
            m = ((p + 1) // 2 + N // 2 * int(rng.integers(0, 2))) % N
            if m == p: m = (m + N // 2) % N
        v[m][:, j] = 2.0 ** -4 * (1 + rng.random((128, 4))) * s * on
        v[p][:, j] = (2.0 ** 5 if p % 2 else -2.0 ** 5) * (1 + rng.random((128, 4))) * s
    return draw(rng, v, q)
def setup_inputs_one(rng):
    v, q = striped(data(rng)), queries(rng)
    s = np.where(q[0, :, :4].astype(np.float32) < 0, -1.0, 1.0)
    q[:, :, 4:8] = (np.abs(q[:, :, 4:8].astype(np.float32)) * s).astype(BF)
    m, i = int(rng.integers(0, N)), np.arange(P)
    at = rng.permutation(np.flatnonzero((i % N != m) & ((i - m + 1) % N != m)))[:2 * K]
    size = np.repeat([2.0 ** 16, 2.0 ** 11], K)
    v[m][:, at] = (1 + rng.random((128, 2 * K, 4))) * s[:, None] * size[:, None]
    return draw(rng, v, q)
def setup_inputs_spread(rng):
    q = (queries(rng).astype(np.float32) * np.float32(2.0 ** 20)).astype(BF)
    return draw(rng, wide(rng, N, 128, 4 * P, cols=6), q)
def setup_inputs_ties(rng):
    v, q = np.zeros((N, 128, P, 4), np.float32), queries(rng)
    s = np.where(q[0, :, 4:8].astype(np.float32) < 0, -1.0, 1.0)
    q[:, :32, :4] = 0
    on = (np.arange(128) < 32)[:, None]
    for p in range(N):
        at = p + N * rng.permutation(P // N)
        for g in range(P // N // 3):
            x = 2.0 ** -2 * rng.standard_normal((N, 128, 1, 4))
            a, b, m = (p + 1 + rng.permutation(N - 1)[:3]) % N
            x[p] *= 2.0 ** 22
            x[m] = x[p]
            x[a, :, 0] = np.where(on, 2.0 ** 23 * (1 + rng.random((128, 4))) * s, x[a, :, 0])
            x[b] = x[a] * rng.choice([-1.0, 1.0])
            v[:, :, at[3 * g:3 * g + 3]] = x * rng.choice([-1.0, 1.0], (3, 1))
    return draw(rng, v, q)
def setup_inputs_zero(rng):
    v = striped(data(rng))
    lo, hi = int(rng.integers(0, K // 4 + 1)), int(rng.integers(K // 2, P - K // 4 + 1))
    v[:, :, :hi] = 0
    v[:, :, hi + K // 4:] = 0
    for j in range(lo, lo + K // 4):
        m, n = (j + 1 + rng.permutation(N - 1)[:2]) % N
        v[m][:, j] = 4 * rng.standard_normal((128, 4))
        v[n][:, j] = -v[m][:, j]
    harm(rng, v, np.arange(hi, hi + K // 4), 8)
    return draw(rng, v)
def check_inputs(d):
    b = []
    for k, lo, hi in (("tb", -16, 24), ("u", -30, 30), ("w", -30, 30)):
        v = np.abs(d[k].astype(np.float32))
        if not (np.isfinite(v).all() and ((v == 0) | (v >= 2.0 ** lo) & (v <= 2.0 ** hi)).all()): b.append("a value of " + k)
    q = d["u"].astype(np.float32)
    if (q[:, :, 8:] != 0).any(): b.append("u has numbers behind its first 2 columns")
    if (q != q[:1]).any(): b.append("u isn't the same on all ranks")
    return b
def reference(tb, u, w):
    tab = [mx_ref.quantize(np.ascontiguousarray(tb[r])) for r in range(N)]
    bs = np.zeros((N, 4, K), np.float32)
    for t in range(2):
        c, g = checks(tab, u)
        bad, lost = judge(c, g, t)
        new = rebuilt(tab, bad, lost, t)
        at = places(t, bad)
        for r in range(N):
            e = np.flatnonzero(lost == r)
            tab[r] = put(tab[r], at[r, e], pick(new, e))
        bs[:, 2 * t] = bad
        bs[:, 2 * t + 1] = lost
    oc, osc, y = np.zeros((N, 128, 4 * P), np.uint8), np.zeros((N, 16, P), np.uint8), np.zeros((N, 128, O * P), np.float32)
    for r in range(N):
        oc[r], osc[r] = emit(tab[r])
        for o in range(O):
            y[r, :, o * P:o * P + P] = mx_ref.matmul(mx_ref.quantize(np.ascontiguousarray(cut(w[r], o))), tab[r])
    return {"oc": oc, "osc": osc, "bs": bs, "y": y}

@@ -1,0 +1,496 @@
+from concourse.bass import DstId, RemoteDMATransfer
+from concourse.mybir import dt, AluOpType, AxisListType, ActivationFunctionType
+
+OP = AluOpType
+AF = ActivationFunctionType
+X = AxisListType.X
+N, P, K, NO, KO = 8, 256, 64, 4, 16
+STEP = 1.0 - 2.0 ** -24
+TINY = 2.0 ** -118
+FR = 2.0 ** -10
+
+F4 = "float8_e4m3fn_x4"
+SCRATCH = {}
+VIEW = {}
+
+
+def _sb(name, n, ty="float32"):
+    SCRATCH[name] = ("sbuf", [128, n], ty)
+
+
+def _mx(name, n):
+    _sb(name, n, F4)
+    _sb(name + "s", n, "uint8")
+
+
+def _parts(buf, *parts):
+    c = 0
+    for name, n in parts:
+        VIEW[name] = (buf, c)
+        c += n + -n % 4
+    _sb(buf, c)
+
+
+for _n, _w in (("tbt", 4 * P), ("ut", 512), ("wt", 512), ("ee", 528), ("zt", 512)):
+    _sb(_n, _w, "bfloat16")
+_parts("con", ("rc", 16), ("r8", 16), ("jc", 2), ("ad", 4), ("ad2", 4), ("hb", 64), ("hx", 32), ("hp", 32), ("hq", 32), ("hr", 32),
+       ("kl0", 8), ("dk", 4), ("dl0", 8), ("fb", 5), ("sd16", 16), ("one", 32), ("oc", 8), ("klc", 8), ("dkw", 4), ("ng", 4),
+       ("ae", 4), ("ma0", 16), ("ma1", 16), ("mb0", 16), ("mb1", 16))
+for _n, _w in (("nat", 528), ("ea", 528), ("x16", 256), ("xa", 256), ("q8", 264), ("qn", 256), ("jp", 256), ("md0", 256), ("md1", 256),
+               ("vj", 128), ("mk", 256), ("sd", 256), ("dpat", 128), ("yb", 256)):
+    _sb(_n, _w)
+_sb("pi", 2, "int32")
+_sb("ib", 5, "int32")
+_sb("cl", 2, "uint16")
+_sb("dl", 8, "uint16")
+for _n, _w in (("tA", P), ("tB", P), ("F", P), ("uq", 128), ("wq", 128), ("eq", 512)):
+    _mx(_n, _w)
+for _t in "01":
+    _parts("jd" + _t, ("d1" + _t, 32), ("so" + _t, 32), ("du" + _t, 64), ("lw" + _t, 64), ("ev" + _t, 32), ("tl" + _t, 64), ("rk" + _t, 2), ("tt" + _t, 128),
+           ("xb" + _t, 4), ("jf" + _t, 4), ("fr" + _t, 4), ("ol" + _t, 128), ("w" + _t, 160), ("th" + _t, 512), ("cm" + _t, 512),
+           ("cj" + _t, 512), ("mm" + _t, 512))
+    for _n, _w in (("L", 32), ("S", 256), ("Lz", 256), ("D", 256), ("dd", 128), ("bk", 64), ("lk", 64), ("lr", 64), ("qk", 64), ("M", 384)):
+        _sb(_n + _t, _w)
+    for _n, _w in (("R", 8), ("of", 4), ("op", 4), ("oo", 2), ("mo", 4), ("ml", 16), ("oi", 8)):
+        _sb(_n + _t, _w, "uint16")
+    _sb("h" + _t, 512, "bfloat16")
+    for _n, _w in (("slot", K), ("land", 256), ("ord", 128), ("new", 128), ("W", P + K)):
+        _mx(_n + _t, _w)
+SCRATCH["pc"] = ("psum", [128, 1024], "float32")
+SCRATCH["dec"] = ("psum", [128, 2048], "float32")
+SCRATCH["py"] = ("psum", [128, 1024], "float32")
+PSUM = ("pc", "dec", "py")
+
+SEMAPHORES = ["qv", "qs", "qt", "qg", "out", "ld_u", "ld_a", "ld_b", "ld_w", "st_c", "st_s", "st_y",
+              "st_b0", "st_b1", "ck0", "ck1", "col0", "col1", "new0", "new1"]
+
+
+def rank_program(g, core, T, topo):
+    rank = T.rank_of(core)
+    if rank is None:
+        return
+    eng = {"v": g.vector, "s": g.scalar, "t": g.tensor, "g": g, "y": g.sync}
+    count = {"v": 0, "s": 0, "t": 0, "g": 0}
+    seen = {e: {} for e in eng}
+    wrote, read = {}, {}
+    final = {}
+
+    def A(name, c0, c1, st=1, p0=0, p1=128):
+        if name in VIEW:
+            name, c = VIEW[name]
+            c0, c1 = c0 + c, c1 + c
+        ap = T[name][p0:p1, c0:c1] if st == 1 else T[name][p0:p1, c0:c1:st]
+        cols = frozenset(c // 512 for c in range(c0, c1, st)) if name in PSUM else frozenset(range(c0, c1, st))
+        return (name, p0, p1, cols, ap)
+
+    def hits(table, r):
+        for (p0, p1, cols, tok) in table.get(r[0], ()):
+            if p0 < r[2] and r[1] < p1 and not cols.isdisjoint(r[3]):
+                yield tok
+
+    def wait(e, sem, val):
+        if seen[e].get(sem, 0) < val:
+            eng[e].wait_ge(T.sem[sem], val)
+            seen[e][sem] = val
+
+    def order(e, ins, outs):
+        need = {}
+        for rs, table, same in ((ins, wrote, True), (outs, wrote, True), (outs, read, False)):
+            for r in rs:
+                for sem, val, src in hits(table, r):
+                    if src != e or (same and r[0] not in PSUM) or rs is ins:
+                        need[sem] = max(need.get(sem, 0), val)
+        for sem, val in need.items():
+            wait(e, sem, val)
+
+    def note(ins, outs, tok):
+        for r in ins:
+            read.setdefault(r[0], []).append((r[1], r[2], r[3], tok))
+        for r in outs:
+            wrote.setdefault(r[0], []).append((r[1], r[2], r[3], tok))
+
+    def op(e, outs, ins, call):
+        order(e, ins, outs)
+        inst = call()
+        count[e] += 1
+        inst.then_inc(T.sem["q" + e], 1)
+        final["q" + e] = count[e]
+        note(ins, outs, ("q" + e, count[e], e))
+
+    def dma(e, out, in_, sem, total, out_ap=None, in_ap=None):
+        order(e, [in_] if in_ else [], [out] if out else [])
+        o = out_ap if out_ap is not None else out[4]
+        i = in_ap if in_ap is not None else in_[4]
+        eng[e].dma_start(o, i).then_inc(T.sem[sem], 16)
+        final[sem] = total
+        note([in_] if in_ else [], [out] if out else [], (sem, total, "dma"))
+
+    def tt(out, a, b, o):
+        op("v", [out], [a, b], lambda: g.vector.tensor_tensor(out[4], a[4], b[4], o))
+
+    def ts(out, a, s1, s2, o0, o1=None):
+        ins = [a] + [s for s in (s1, s2) if isinstance(s, tuple)]
+        v1 = s1[4] if isinstance(s1, tuple) else s1
+        v2 = s2[4] if isinstance(s2, tuple) else s2
+        if o1 is None:
+            op("v", [out], ins, lambda: g.vector.tensor_scalar(out[4], a[4], v1, None, o0))
+        else:
+            op("v", [out], ins, lambda: g.vector.tensor_scalar(out[4], a[4], v1, v2, o0, o1))
+
+    def act(out, a, f, bias=None, scale=None):
+        ins = [a] + [s for s in (bias, scale) if isinstance(s, tuple)]
+        kw = {}
+        if bias is not None:
+            kw["bias"] = bias[4] if isinstance(bias, tuple) else bias
+        if scale is not None:
+            kw["scale"] = scale[4] if isinstance(scale, tuple) else scale
+        op("s", [out], ins, lambda: g.scalar.activation(out[4], a[4], f, **kw))
+
+    def cp(e, out, a):
+        if e == "v":
+            op("v", [out], [a], lambda: g.vector.tensor_copy(out[4], a[4]))
+        else:
+            act(out, a, AF.Copy)
+
+    def fill(out, x):
+        op("v", [out], [], lambda: g.vector.memset(out[4], x))
+
+    def red(out, a, o):
+        op("v", [out], [a], lambda: g.vector.tensor_reduce(out[4], a[4], X, o))
+
+    def scan(out, d0, d1, o0, o1):
+        op("v", [out], [d0, d1], lambda: g.vector.tensor_tensor_scan(out[4], d0[4], d1[4], 0.0, o0, o1))
+
+    def turn(out, a):
+        op("v", [out], [a], lambda: g.vector.transpose(out[4], a[4]))
+
+    part = [False]
+
+    def iota(out, pat, base, cm, flag=True):
+        kw = {"allow_small_or_imprecise_dtypes": True} if flag else {}
+        now = out[1] != 0 or out[2] != 128
+        if now or part[0]:
+            wait("g", "qg", count["g"])
+        part[0] = now
+        op("g", [out], [], lambda: g.iota(out[4], pat, base, cm, **kw))
+
+    def gather(e, out, win, off):
+        if e == "v":
+            op("v", [out], [win, off], lambda: g.vector.tensor_copy(out[4], win[4].indirect(off[4])))
+        else:
+            op("s", [out], [win, off], lambda: g.scalar.activation(out[4], win[4].indirect(off[4]), AF.Copy))
+
+    def scatter(win, off, val):
+        op("v", [win], [val, off], lambda: g.vector.tensor_copy(win[4].indirect(off[4]), val[4]))
+
+    def pick(dst, c0, c1, src, n, off):
+        o, i = A(dst, c0, c1), A(src, 0, n)
+        op("v", [o], [i, off], lambda: g.vector.tensor_copy(o[4].bitcast(dt.uint32), i[4].bitcast(dt.uint32).indirect(off[4])))
+        gather("s", A(dst + "s", c0, c1), A(src + "s", 0, n), off)
+
+    def quant(dst, c0, c1, tile, a0):
+        o, s, i = A(dst, c0, c1), A(dst + "s", c0, c1), A(tile, a0, a0 + 4 * (c1 - c0))
+        op("v", [o, s], [i], lambda: g.vector.quantize_mx(o[4], s[4], i[4]))
+
+    def mm(out, lhs, a, rhs, b0, b1):
+        l, ls, r, rs = A(lhs, a, a + 128), A(lhs + "s", a, a + 128), A(rhs, b0, b1), A(rhs + "s", b0, b1)
+        op("t", [out], [l, ls, r, rs], lambda: g.tensor.matmul_mx(out[4], l[4], ls[4], r[4], rs[4], True, True))
+
+    peers = [c for c in T.cores if c != core]
+
+    def dest(c):
+        rid, pid, _s = topo.addr(c)
+        return DstId(rid=rid, pnc=pid)
+
+    def raw(r, codes):
+        return r[4].bitcast(dt.uint8) if codes else r[4]
+
+    def spread(ref, sem, codes=False):
+        order("g", [ref], [])
+        m = topo.mask(core, peers[0])
+        for c in peers:
+            m &= topo.mask(core, c)
+        g.remote_dma_fused([RemoteDMATransfer(dst_ids=[dest(c) for c in peers], dma_engine_mask=m, remote_sem=T.sem[sem],
+                                              srcs=[raw(ref, codes)], dsts=[raw(ref, codes) for _ in peers])],
+                           local_sem=T.sem["out"])
+        final["out"] = final.get("out", 0) + bin(m).count("1")
+
+    full = len(topo.engines(core, peers[0]))
+
+    def deal(t, codes):
+        tr = []
+        for o in range(NO):
+            c = T.cores[2 * o + t]
+            if c == core:
+                continue
+            es = topo.engines(core, c)
+            w = len(es) // NO
+            s = "" if codes else "s"
+            src = A("slot%d" % t + s, KO * o, KO * o + KO)
+            order("g", [src], [])
+            d = A("land%d" % t + s, KO * rank, KO * rank + KO)
+            tr.append(RemoteDMATransfer(dst_ids=[dest(c)], dma_engine_mask=sum(1 << e for e in es[w * o:w * o + w]),
+                                        remote_sem=T.sem["col%d" % t], srcs=[raw(src, codes)], dsts=[raw(d, codes)]))
+            final["out"] = final.get("out", 0) + w
+        g.remote_dma_fused(tr, local_sem=T.sem["out"])
+
+    own = rank % 2
+    o_ = rank // 2
+
+    dma("y", A("tbt", 0, 512), None, "ld_a", 16, in_ap=T.tb[:, 0:512])
+    dma("s", A("ut", 0, 8), None, "ld_u", 16, in_ap=T.u[:, 0:8])
+    dma("s", A("tbt", 512, 1024), None, "ld_b", 16, in_ap=T.tb[:, 512:1024])
+    dma("y", A("wt", 0, 512), None, "ld_w", 16, in_ap=T.w[:])
+
+    iota(A("pi", 0, 2), [[1, 2]], 0, 1, False)
+    iota(A("rc", 0, 16), [[1, 8], [0, 2]], 0, 0)
+    iota(A("nat", 0, 128), [[1, 128]], 0, 0)
+    iota(A("jc", 0, 2), [[128, 2]], 0, 1)
+    iota(A("hb", 0, 64), [[128, 2], [1, 32]], 0, 0)
+    iota(A("hx", 0, 32), [[128, 2], [1, 16]], 0, 0)
+    iota(A("hp", 0, 32), [[32, 2], [1, 16]], 0, 0)
+    iota(A("r8", 0, 16), [[0, 2], [1, 8]], -8, 0)
+    iota(A("dl0", 0, 8), [[16, 4], [0, 2]], 0, 0)
+    for a in range(4):
+        iota(A("ad", 0, 4, 1, 32 * a, 32 * a + 32), [[32 * ((a ^ 1) - a), 2], [32 * ((a ^ 2) - a), 2]], 32 * a, 0)
+    fill(A("ut", 8, 512), 0.0)
+    fill(A("one", 0, 32), 1.0)
+    fill(A("sd16", 1, 16), 1.0)
+    fill(A("sd16", 0, 1), 0.0)
+    for col, (src, bits) in enumerate(((0, 7), (1, 7), (0, 16), (0, 15), (0, 8))):
+        ts(A("ib", col, col + 1), A("pi", src, src + 1), bits, None, OP.bitwise_and)
+    cp("v", A("fb", 0, 5), A("ib", 0, 5))
+    for t in range(2):
+        ts(A("ma%d" % t, 0, 16), A("rc", 0, 16), A("fb", t, t + 1), -1.0, OP.is_equal, OP.mult)
+        ts(A("mb%d" % t, 0, 16), A("rc", 0, 16), A("fb", t, t + 1), None, OP.not_equal)
+    ts(A("ng", 0, 1), A("jc", 0, 1), -4.0, -4.0, OP.mult, OP.add)
+    ts(A("ng", 1, 2), A("fb", 3, 4), -1.0, None, OP.mult)
+    quant("uq", 0, 128, "ut", 0)
+    act(A("nat", 128, 256), A("nat", 0, 128), AF.Identity, bias=128.0)
+    act(A("nat", 256, 512), A("nat", 0, 256), AF.Identity, bias=256.0)
+    act(A("nat", 512, 528), A("nat", 0, 16), AF.Identity, bias=512.0)
+    act(A("D0", 0, 256), A("nat", 0, 256), AF.Copy, scale=0.0)
+
+    def checks(t, tab, halves):
+        for h in range(2):
+            halves(h)
+            mm(A("pc", 512 * h, 512 * h + 128), tab, 128 * h, "uq", 0, 128)
+        for h, e in ((0, "s"), (1, "v")):
+            cp(e, A("L%d" % t, 4 * rank + 2 * h, 4 * rank + 2 * h + 2), A("pc", 512 * h, 512 * h + 2))
+        spread(A("L%d" % t, 4 * rank, 4 * rank + 4), "ck%d" % t)
+        for r in range(N):
+            if r != rank:
+                note([], [A("L%d" % t, 4 * r, 4 * r + 4)], ("ck%d" % t, 7 * full, "remote"))
+        final["ck%d" % t] = 7 * full
+
+    checks(0, "tA", lambda h: quant("tA", 128 * h, 128 * h + 128, "tbt", 512 * h))
+
+    for s in range(4):
+        ts(A("jp", 64 * s, 64 * s + 64), A("hb", 0, 64), A("ad", s, s + 1), None, OP.add)
+    ts(A("ad2", 0, 1), A("fb", 2, 3), 1.0 + FR, None, OP.mult)
+    ts(A("hq", 0, 32), A("hp", 0, 32), FR, None, OP.mult)
+    for h in range(2):
+        ts(A("md%d" % h, 0, 256), A("jp", 0, 256), A("jc", h, h + 1), STEP, OP.is_ge, OP.max)
+    tt(A("hr", 0, 32), A("hq", 0, 32), A("hx", 0, 32), OP.add)
+    ts(A("ae", 0, 4), A("ad", 0, 4), A("ad2", 0, 1), None, OP.add)
+    for s in range(4):
+        ts(A("vj", 32 * s, 32 * s + 32), A("hr", 0, 32), A("ae", s, s + 1), 64.0 * FR * s, OP.add, OP.add)
+    ts(A("dl", 0, 8), A("dl0", 0, 8), A("fb", 3, 4), None, OP.add)
+    iota(A("x16", 0, 256), [[0, 16], [1, 16]], 0, 0)
+    iota(A("q8", 0, 264), [[0, 33], [1, 8]], 0, 0)
+    iota(A("kl0", 0, 8), [[2, 8]], 0, 0)
+    iota(A("dk", 0, 4), [[16, 4]], P + K, 0)
+    act(A("ea", 0, 528), A("nat", 0, 528), AF.Abs, bias=A("ng", 0, 1))
+    act(A("ee", 0, 528), A("ea", 0, 528), AF.Relu, bias=1.0, scale=-1.0)
+    act(A("zt", 0, 512), A("nat", 0, 512), AF.Copy, scale=0.0)
+    act(A("xa", 0, 256), A("x16", 0, 256), AF.Abs, bias=A("ng", 1, 2))
+    act(A("mk", 0, 256), A("xa", 0, 256), AF.Relu, bias=1.0, scale=-1.0)
+    act(A("sd", 0, 256), A("x16", 0, 256), AF.Sign)
+    cp("s", A("qn", 0, 256), A("q8", own, own + 256))
+    fill(A("dpat", 0, 128), 1.0)
+    ts(A("oc", 0, 1), A("fb", 0, 1), -1.0, None, OP.add)
+    ts(A("oc", 1, 2), A("fb", 0, 1), -1.0, 0.0, OP.add, OP.max)
+    ts(A("oc", 2, 3), A("fb", 0, 1), 0.0, None, OP.is_equal)
+    fill(A("dpat", 0, 128, 8), 0.0)
+    fill(A("dpat", 1, 128, 8), -1.0)
+    ts(A("oc", 3, 4), A("fb", 4, 5), 0.125, None, OP.mult)
+    ts(A("oc", 4, 5), A("fb", 4, 5), 12.5, -8.0, OP.mult, OP.add)
+    ts(A("oc", 5, 6), A("fb", 4, 5), -12.5, 92.0, OP.mult, OP.add)
+    ts(A("cl", 0, 1), A("fb", 3, 4), 8.0, 7.0, OP.mult, OP.add)
+    ts(A("klc", 0, 8), A("kl0", 0, 8), A("oc", 3, 4), 1.0 / 128, OP.add, OP.mult)
+    ts(A("dkw", 0, 4), A("dk", 0, 4), A("fb", 3, 4), None, OP.add)
+    for b in range(4):
+        quant("eq", 128 * b, 128 * b + 128, "ee", 4 - b)
+    quant("land%d" % own, 128, 256, "zt", 0)
+    quant("W0", 0, 256, "tbt", 0)
+
+    def across(buf, e1, e2):
+        cp(e1, A(buf, 64, 128, 1, 0, 64), A(buf, 0, 64, 1, 64, 128))
+        cp(e2, A(buf, 64, 128, 1, 64, 128), A(buf, 0, 64, 1, 0, 64))
+        for a in range(4):
+            b = a ^ 1
+            cp("s", A(buf, 128, 256, 1, 32 * a, 32 * a + 32), A(buf, 0, 128, 1, 32 * b, 32 * b + 32))
+
+    def judge(t, tab):
+        n = lambda s: s + str(t)
+        L, d1, so, du, S, lw, ev, tl = n("L"), n("d1"), n("so"), n("du"), n("S"), n("lw"), n("ev"), n("tl")
+        act(A(lw, 0, 16), A(L, 1, 32, 2), AF.Abs)
+        tt(A(d1, 0, 16), A(L, 0, 32, 2), A(n("ma"), 0, 16), OP.mult)
+        tt(A(d1, 16, 32), A(L, 0, 32, 2), A(n("mb"), 0, 16), OP.mult)
+        for h in range(2):
+            scan(A(so, 16 * h, 16 * h + 16), A("sd16", 0, 16), A(d1, h, 32, 2), OP.mult, OP.subtract)
+        for h in range(2):
+            act(A(du, 32 * h, 32 * h + 32), A("one", 0, 32), AF.Abs, bias=TINY, scale=A(so, 16 * h + 15, 16 * h + 16))
+        tt(A(lw, 16, 32), A(lw, 0, 16), A(n("mb"), 0, 16), OP.mult)
+        tt(A(lw, 32, 48), A(lw, 16, 32), A(n("ma"), 0, 16), OP.add)
+        turn(A(S, 0, 64), A(du, 0, 64))
+        across(S, "v", "s")
+        for h in range(2):
+            ts(A(n("th"), 256 * h, 256 * h + 256), A("md%d" % h, 0, 256), A(du, 32 * h, 32 * h + 1), None, OP.mult)
+        for h in range(2):
+            red(A(lw, 48 + h, 49 + h), A(lw, 32 + h, 48, 2), OP.max)
+        for h in range(2):
+            tt(A(n("cm"), 256 * h, 256 * h + 256), A(S, 0, 256), A(n("th"), 256 * h, 256 * h + 256), OP.is_gt)
+        for h in range(2):
+            o, i, c = A(n("cj"), 256 * h, 256 * h + 256), A(n("cm"), 256 * h, 256 * h + 256), A(n("rk"), h, h + 1)
+            op("s", [o, c], [i], lambda o=o, i=i, c=c: g.scalar.activation(o[4], i[4], AF.Copy, accum_out=c[4]))
+        for h in range(2):
+            ts(A(ev, 8 * h, 8 * h + 8), A(lw, 32 + h, 48, 2), A(lw, 48 + h, 49 + h), None, OP.is_equal)
+        R, rk = n("R"), n("rk")
+        cp("v", A(R, 0, 2), A(rk, 0, 2))
+        cp("v", A(R, 2, 4, 1, 0, 64), A(rk, 0, 2, 1, 64, 128))
+        cp("v", A(R, 2, 4, 1, 64, 128), A(rk, 0, 2, 1, 0, 64))
+        tt(A(ev, 16, 32), A(ev, 0, 16), A("r8", 0, 16), OP.mult)
+        for a in range(4):
+            b = a ^ 1
+            cp("v", A(R, 4, 8, 1, 32 * a, 32 * a + 32), A(R, 0, 4, 1, 32 * b, 32 * b + 32))
+        scatter(A(n("D"), 0, 256), A(R, 0, 8), A("vj", 0, 128))
+        red(A(lw, 50, 51), A(ev, 16, 24), OP.min)
+        gather("v", A(n("dd"), 0, 128), A(n("D"), 0, 64), A("dl", 0, 8))
+        red(A(lw, 51, 52), A(ev, 24, 32), OP.min)
+        for h in range(2):
+            act(A(tl, 32 * h, 32 * h + 32), A("one", 0, 32), AF.Copy, scale=A(lw, 50 + h, 51 + h))
+        turn(A(n("tt"), 0, 128), A(n("dd"), 0, 128))
+        xb, of = n("xb"), n("of")
+        tt(A(xb, 0, 4), A(n("tt"), 0, 128, 32), A(n("tt"), 16, 128, 32), OP.add)
+        cp("v", A(of, 0, 4), A(xb, 0, 4))
+        pick(n("slot"), 0, K, tab, P, A(of, 0, 4))
+        deal(t, True)
+        deal(t, False)
+        turn(A(n("Lz"), 0, 64), A(tl, 0, 64))
+        across(n("Lz"), "v", "s")
+        if own == t:
+            cp("v", A(n("oo"), 0, 1), A(xb, o_, o_ + 1))
+            pick(n("land"), KO * rank, KO * rank + KO, tab, P, A(n("oo"), 0, 1))
+        cp("v", A(n("jf"), 0, 4), A(of, 0, 4))
+        tt(A(n("fr"), 0, 4), A(xb, 0, 4), A(n("jf"), 0, 4), OP.subtract)
+        ts(A(n("op"), 0, 4), A(n("fr"), 0, 4), 1.0 / FR, None, OP.mult)
+        if own == t:
+            gather("v", A(n("qk"), 0, 64), A("qn", 0, 256), A(of, 0, 4))
+
+    def lists(t):
+        n = lambda s: s + str(t)
+        gather("s", A(n("bk"), 0, 64), A("nat", 0, 256), A(n("of"), 0, 4))
+        act(A(n("lr"), 0, 64), A(n("lk"), 0, 64), AF.Identity, bias=8.0)
+        dma("y", None, A(n("bk"), 0, 64, 1, 0, 1), "st_b%d" % t, 32, out_ap=T.bs[2 * t:2 * t + 1, :])
+        dma("y", None, A(n("lr"), 0, 64, 1, 0, 1), "st_b%d" % t, 32, out_ap=T.bs[2 * t + 1:2 * t + 2, :])
+
+    def lostlist(t):
+        n = lambda s: s + str(t)
+        gather("v", A(n("lk"), 0, 64), A(n("Lz"), 0, 256), A(n("op"), 0, 4))
+
+    def rebuild(t):
+        n = lambda s: s + str(t)
+        ol, a0, qk, lk = n("ol"), KO * o_, n("qk"), n("lk")
+        v = lambda i: A(ol, 8 * i, 8 * i + 8)
+        even = A(qk, a0, a0 + 16, 2)
+        tt(v(0), A(qk, a0 + 1, a0 + 16, 2), even, OP.subtract)
+        ts(v(1), v(0), A("oc", 3, 4), None, OP.mult)
+        tt(v(2), v(1), even, OP.add)
+        ts(v(3), v(2), A("oc", 0, 1), None, OP.is_le)
+        ts(v(4), v(2), A("oc", 2, 3), A("oc", 1, 2), OP.mult, OP.add)
+        tt(v(5), v(3), v(4), OP.add)
+        ts(v(6), v(5), A("oc", 4, 5), None, OP.add)
+        ts(v(7), v(5), A("oc", 5, 6), None, OP.add)
+        ts(v(8), v(5), KO / 128.0, None, OP.mult)
+        tt(v(9), v(8), A("klc", 0, 8), OP.add)
+        lostlist(t)
+        tt(v(10), v(6), A(lk, a0, a0 + 16, 2), OP.is_equal)
+        tt(v(11), v(7), A(lk, a0 + 1, a0 + 16, 2), OP.is_equal)
+        tt(v(12), v(9), v(10), OP.add)
+        tt(v(13), v(12), v(11), OP.add)
+        ts(A(n("oi"), 0, 8), v(13), 128.0, None, OP.mult)
+        tot = 7 * 2 * (full // NO)
+        for r in range(N):
+            if r != rank:
+                for s in ("", "s"):
+                    note([], [A(n("land") + s, KO * r, KO * r + KO)], ("col%d" % t, tot, "remote"))
+        final["col%d" % t] = tot
+        pick(n("ord"), 0, 128, n("land"), 256, A(n("oi"), 0, 8))
+        for b in range(4):
+            mm(A("dec", 512 * b, 512 * b + 128), "eq", 128 * b, n("ord"), 0, 128)
+        for b in range(4):
+            scan(A(n("h"), b, 512, 4), A("dpat", 0, 128), A("dec", 512 * b, 512 * b + 128), OP.mult, OP.subtract)
+        quant(n("new"), 0, 128, n("h"), 0)
+        pick(n("W"), P + a0, P + a0 + KO, n("new"), 128, A("cl", 0, 1))
+        spread(A(n("W"), P + a0, P + a0 + KO), "new%d" % t, True)
+        spread(A(n("W") + "s", P + a0, P + a0 + KO), "new%d" % t)
+
+    def newlist(t):
+        n = lambda s: s + str(t)
+        w, mo = n("w"), n("mo")
+        tt(A(w, 0, 64), A(n("lk"), 0, 64), A("mk", 0, 64), OP.mult)
+        tt(A(w, 136, 140), A(n("jf"), 0, 4), A("dkw", 0, 4), OP.subtract)
+        scan(A(w, 64, 128), A("sd", 0, 64), A(w, 0, 64), OP.mult, OP.add)
+        ts(A(w, 132, 136), A(w, 79, 128, 16), float(rank - 8), None, OP.is_equal)
+        tt(A(w, 140, 144), A(w, 132, 136), A(w, 136, 140), OP.mult)
+        tt(A(w, 144, 148), A(w, 140, 144), A("dkw", 0, 4), OP.add)
+        cp("v", A(mo, 0, 4), A(w, 144, 148))
+        scatter(A(n("M"), 0, 384), A(mo, 0, 4), A("nat", P, P + K))
+        m, mmx = n("M"), n("mm")
+        cut = rank if t == 0 else P - rank if rank else 0
+        tt(A(mmx, 0, P - cut), A(m, cut, P), A("mk", 0, P - cut), OP.mult)
+        if cut:
+            tt(A(mmx, P - cut, P), A(m, 0, cut), A("mk", P - cut, P), OP.mult)
+        scan(A(mmx, 256, 512), A("sd", 0, 256), A(mmx, 0, 256), OP.mult, OP.add)
+        cp("v", A(n("ml"), 0, 16), A(mmx, 256 + 15, 512, 16))
+
+    def arrive(t):
+        n = lambda s: s + str(t)
+        others = [o for o in range(NO) if 2 * o + t != rank]
+        tot = len(others) * 2 * full
+        for o in others:
+            for s in ("", "s"):
+                note([], [A(n("W") + s, P + KO * o, P + KO * o + KO)], ("new%d" % t, tot, "remote"))
+        final["new%d" % t] = tot
+
+    def finish(t):
+        cp("s", A("M%d" % t, 0, 384), A("nat", 0, 384))
+        if own == t:
+            rebuild(t)
+        else:
+            lostlist(t)
+        lists(t)
+        newlist(t)
+        arrive(t)
+
+    judge(0, "tA")
+    finish(0)
+    act(A("D1", 0, 256), A("nat", 0, 256), AF.Copy, scale=0.0)
+    checks(1, "tB", lambda h: pick("tB", 128 * h, 128 * h + 128, "W0", P + K, A("ml0", 8 * h, 8 * h + 8)))
+    pick("W1", 0, P, "W0", P + K, A("ml0", 0, 16))
+    quant("wq", 0, 128, "wt", 0)
+    judge(1, "tB")
+    finish(1)
+    for h in range(2):
+        pick("F", 128 * h, 128 * h + 128, "W1", P + K, A("ml1", 8 * h, 8 * h + 8))
+        mm(A("py", 512 * h, 512 * h + 128), "wq", 0, "F", 128 * h, 128 * h + 128)
+    cp("s", A("yb", 0, 128), A("py", 0, 128))
+    cp("v", A("yb", 128, 256), A("py", 512, 640))
+    dma("y", None, A("F", 0, P), "st_c", 16, out_ap=T.oc[:], in_ap=T.F[:, 0:P].bitcast(dt.uint8))
+    dma("y", None, A("yb", 0, 128), "st_y", 32, out_ap=T.y[:, 0:128])
+    dma("s", None, A("yb", 128, 256), "st_y", 32, out_ap=T.y[:, 128:256])
+    for k in range(4):
+        dma("s" if k % 2 else "y", None, A("Fs", 0, P, 1, 32 * k, 32 * k + 4), "st_s", 64, out_ap=T.osc[4 * k:4 * k + 4, :])
+    for sem, val in final.items():
+        wait("g", sem, val)

@@ -34,8 +34,8 @@ def _parts(buf, *parts):
 for _n, _w in (("tbt", 4 * P), ("ut", 512), ("wt", 512), ("ee", 528), ("zt", 512)):
     _sb(_n, _w, "bfloat16")
 _parts("con", ("rc", 16), ("r8", 16), ("jc", 2), ("ad", 4), ("ad2", 4), ("hb", 64), ("hx", 32), ("hp", 32), ("hq", 32), ("hr", 32),
-       ("kl0", 8), ("dk", 4), ("dl0", 8), ("fb", 5), ("sd16", 16), ("one", 32), ("oc", 8), ("klc", 8), ("dkw", 4), ("ng", 4),
-       ("ae", 4), ("ma0", 16), ("ma1", 16), ("mb0", 16), ("mb1", 16))
+       ("kl0", 8), ("dk", 4), ("dl0", 8), ("fb", 5), ("sd16", 16), ("one", 32), ("oc", 8), ("klc", 8),
+       ("dkw", 4), ("ng", 4), ("ae", 4), ("ma0", 16), ("ma1", 16), ("mb0", 16), ("mb1", 16))
 for _n, _w in (("nat", 528), ("ea", 528), ("x16", 256), ("xa", 256), ("q8", 264), ("qn", 256), ("jp", 256), ("md0", 256), ("md1", 256),
                ("vj", 128), ("mk", 256), ("sd", 256), ("dpat", 128), ("yb", 256)):
     _sb(_n, _w)
@@ -46,7 +46,7 @@ _sb("dl", 8, "uint16")
 for _n, _w in (("tA", P), ("tB", P), ("F", P), ("uq", 128), ("wq", 128), ("eq", 512)):
     _mx(_n, _w)
 for _t in "01":
-    _parts("jd" + _t, ("d1" + _t, 32), ("so" + _t, 32), ("du" + _t, 64), ("lw" + _t, 64), ("ev" + _t, 32), ("tl" + _t, 64), ("rk" + _t, 2), ("tt" + _t, 128),
+    _parts("jd" + _t, ("d1" + _t, 32), ("so" + _t, 32), ("du" + _t, 64), ("lw" + _t, 64), ("ev" + _t, 32), ("tl" + _t, 64), ("rk" + _t, 8), ("tt" + _t, 128),
            ("xb" + _t, 4), ("jf" + _t, 4), ("fr" + _t, 4), ("ol" + _t, 128), ("w" + _t, 160), ("th" + _t, 512), ("cm" + _t, 512),
            ("cj" + _t, 512), ("mm" + _t, 512))
     for _n, _w in (("L", 32), ("S", 256), ("Lz", 256), ("D", 256), ("dd", 128), ("bk", 64), ("lk", 64), ("lr", 64), ("qk", 64), ("M", 384)):
@@ -188,8 +188,8 @@ def rank_program(g, core, T, topo):
         op("v", [o], [i, off], lambda: g.vector.tensor_copy(o[4].bitcast(dt.uint32), i[4].bitcast(dt.uint32).indirect(off[4])))
         gather("s", A(dst + "s", c0, c1), A(src + "s", 0, n), off)
 
-    def quant(dst, c0, c1, tile, a0):
-        o, s, i = A(dst, c0, c1), A(dst + "s", c0, c1), A(tile, a0, a0 + 4 * (c1 - c0))
+    def quant(dst, c0, c1, tile, at):
+        o, s, i = A(dst, c0, c1), A(dst + "s", c0, c1), A(tile, at, at + 4 * (c1 - c0))
         op("v", [o, s], [i], lambda: g.vector.quantize_mx(o[4], s[4], i[4]))
 
     def mm(out, lhs, a, rhs, b0, b1):
@@ -217,6 +217,10 @@ def rank_program(g, core, T, topo):
 
     full = len(topo.engines(core, peers[0]))
 
+    def landed(refs, sem, total):
+        note([], refs, (sem, total, "remote"))
+        final[sem] = total
+
     def deal(t, codes):
         tr = []
         for o in range(NO):
@@ -236,10 +240,12 @@ def rank_program(g, core, T, topo):
 
     own = rank % 2
     o_ = rank // 2
+    a0 = KO * o_
 
     dma("y", A("tbt", 0, 512), None, "ld_a", 16, in_ap=T.tb[:, 0:512])
     dma("s", A("ut", 0, 8), None, "ld_u", 16, in_ap=T.u[:, 0:8])
     dma("s", A("tbt", 512, 1024), None, "ld_b", 16, in_ap=T.tb[:, 512:1024])
+    wait("y", "ld_b", 16)
     dma("y", A("wt", 0, 512), None, "ld_w", 16, in_ap=T.w[:])
 
     iota(A("pi", 0, 2), [[1, 2]], 0, 1, False)
@@ -260,9 +266,8 @@ def rank_program(g, core, T, topo):
     for col, (src, bits) in enumerate(((0, 7), (1, 7), (0, 16), (0, 15), (0, 8))):
         ts(A("ib", col, col + 1), A("pi", src, src + 1), bits, None, OP.bitwise_and)
     cp("v", A("fb", 0, 5), A("ib", 0, 5))
-    for t in range(2):
-        ts(A("ma%d" % t, 0, 16), A("rc", 0, 16), A("fb", t, t + 1), -1.0, OP.is_equal, OP.mult)
-        ts(A("mb%d" % t, 0, 16), A("rc", 0, 16), A("fb", t, t + 1), None, OP.not_equal)
+    ts(A("ma0", 0, 16), A("rc", 0, 16), A("fb", 0, 1), -1.0, OP.is_equal, OP.mult)
+    ts(A("mb0", 0, 16), A("rc", 0, 16), A("fb", 0, 1), None, OP.not_equal)
     ts(A("ng", 0, 1), A("jc", 0, 1), -4.0, -4.0, OP.mult, OP.add)
     ts(A("ng", 1, 2), A("fb", 3, 4), -1.0, None, OP.mult)
     quant("uq", 0, 128, "ut", 0)
@@ -271,17 +276,14 @@ def rank_program(g, core, T, topo):
     act(A("nat", 512, 528), A("nat", 0, 16), AF.Identity, bias=512.0)
     act(A("D0", 0, 256), A("nat", 0, 256), AF.Copy, scale=0.0)
 
-    def checks(t, tab, halves):
+    def checks(t, tab, half):
         for h in range(2):
-            halves(h)
+            half(h)
             mm(A("pc", 512 * h, 512 * h + 128), tab, 128 * h, "uq", 0, 128)
         for h, e in ((0, "s"), (1, "v")):
             cp(e, A("L%d" % t, 4 * rank + 2 * h, 4 * rank + 2 * h + 2), A("pc", 512 * h, 512 * h + 2))
         spread(A("L%d" % t, 4 * rank, 4 * rank + 4), "ck%d" % t)
-        for r in range(N):
-            if r != rank:
-                note([], [A("L%d" % t, 4 * r, 4 * r + 4)], ("ck%d" % t, 7 * full, "remote"))
-        final["ck%d" % t] = 7 * full
+        landed([A("L%d" % t, 4 * r, 4 * r + 4) for r in range(N) if r != rank], "ck%d" % t, 7 * full)
 
     checks(0, "tA", lambda h: quant("tA", 128 * h, 128 * h + 128, "tbt", 512 * h))
 
@@ -296,40 +298,45 @@ def rank_program(g, core, T, topo):
     for s in range(4):
         ts(A("vj", 32 * s, 32 * s + 32), A("hr", 0, 32), A("ae", s, s + 1), 64.0 * FR * s, OP.add, OP.add)
     ts(A("dl", 0, 8), A("dl0", 0, 8), A("fb", 3, 4), None, OP.add)
-    iota(A("x16", 0, 256), [[0, 16], [1, 16]], 0, 0)
     iota(A("q8", 0, 264), [[0, 33], [1, 8]], 0, 0)
     iota(A("kl0", 0, 8), [[2, 8]], 0, 0)
+    iota(A("x16", 0, 256), [[0, 16], [1, 16]], 0, 0)
     iota(A("dk", 0, 4), [[16, 4]], P + K, 0)
     act(A("ea", 0, 528), A("nat", 0, 528), AF.Abs, bias=A("ng", 0, 1))
     act(A("ee", 0, 528), A("ea", 0, 528), AF.Relu, bias=1.0, scale=-1.0)
     act(A("zt", 0, 512), A("nat", 0, 512), AF.Copy, scale=0.0)
-    act(A("xa", 0, 256), A("x16", 0, 256), AF.Abs, bias=A("ng", 1, 2))
-    act(A("mk", 0, 256), A("xa", 0, 256), AF.Relu, bias=1.0, scale=-1.0)
-    act(A("sd", 0, 256), A("x16", 0, 256), AF.Sign)
     cp("s", A("qn", 0, 256), A("q8", own, own + 256))
-    fill(A("dpat", 0, 128), 1.0)
-    ts(A("oc", 0, 1), A("fb", 0, 1), -1.0, None, OP.add)
-    ts(A("oc", 1, 2), A("fb", 0, 1), -1.0, 0.0, OP.add, OP.max)
-    ts(A("oc", 2, 3), A("fb", 0, 1), 0.0, None, OP.is_equal)
-    fill(A("dpat", 0, 128, 8), 0.0)
-    fill(A("dpat", 1, 128, 8), -1.0)
-    ts(A("oc", 3, 4), A("fb", 4, 5), 0.125, None, OP.mult)
-    ts(A("oc", 4, 5), A("fb", 4, 5), 12.5, -8.0, OP.mult, OP.add)
-    ts(A("oc", 5, 6), A("fb", 4, 5), -12.5, 92.0, OP.mult, OP.add)
-    ts(A("cl", 0, 1), A("fb", 3, 4), 8.0, 7.0, OP.mult, OP.add)
-    ts(A("klc", 0, 8), A("kl0", 0, 8), A("oc", 3, 4), 1.0 / 128, OP.add, OP.mult)
-    ts(A("dkw", 0, 4), A("dk", 0, 4), A("fb", 3, 4), None, OP.add)
-    for b in range(4):
-        quant("eq", 128 * b, 128 * b + 128, "ee", 4 - b)
-    quant("land%d" % own, 128, 256, "zt", 0)
-    quant("W0", 0, 256, "tbt", 0)
 
-    def across(buf, e1, e2):
-        cp(e1, A(buf, 64, 128, 1, 0, 64), A(buf, 0, 64, 1, 64, 128))
-        cp(e2, A(buf, 64, 128, 1, 64, 128), A(buf, 0, 64, 1, 0, 64))
-        for a in range(4):
-            b = a ^ 1
-            cp("s", A(buf, 128, 256, 1, 32 * a, 32 * a + 32), A(buf, 0, 128, 1, 32 * b, 32 * b + 32))
+    def owner():
+        fill(A("dpat", 0, 128), 1.0)
+        ts(A("oc", 0, 1), A("fb", 0, 1), -1.0, None, OP.add)
+        ts(A("oc", 1, 2), A("fb", 0, 1), -1.0, 0.0, OP.add, OP.max)
+        ts(A("oc", 2, 3), A("fb", 0, 1), 0.0, None, OP.is_equal)
+        fill(A("dpat", 0, 128, 8), 0.0)
+        fill(A("dpat", 1, 128, 8), -1.0)
+        ts(A("oc", 3, 4), A("fb", 4, 5), 0.125, None, OP.mult)
+        ts(A("oc", 4, 5), A("fb", 4, 5), 12.5, -8.0, OP.mult, OP.add)
+        ts(A("oc", 5, 6), A("fb", 4, 5), -12.5, 92.0, OP.mult, OP.add)
+        ts(A("cl", 0, 1), A("fb", 3, 4), 8.0, 7.0, OP.mult, OP.add)
+        ts(A("klc", 0, 8), A("kl0", 0, 8), A("oc", 3, 4), 1.0 / 128, OP.add, OP.mult)
+        quant("land%d" % own, 128, 256, "zt", 0)
+
+    def unit(b):
+        quant("eq", 128 * b, 128 * b + 128, "ee", 4 - b)
+
+    if own == 0:
+        owner()
+
+    def across(buf, v):
+        cp("v", A(buf, 64, 128, 1, 0, 64), A(buf, 0, 64, 1, 64, 128))
+        cp("s", A(buf, 64, 128, 1, 64, 128), A(buf, 0, 64, 1, 0, 64))
+
+        def rest(e, a1, a2):
+            for a in range(a1, a2):
+                b = a ^ 1
+                cp(e, A(buf, 128, 256, 1, 32 * a, 32 * a + 32), A(buf, 0, 128, 1, 32 * b, 32 * b + 32))
+        rest("s", v, 4)
+        return lambda: rest("v", 0, v)
 
     def judge(t, tab):
         n = lambda s: s + str(t)
@@ -344,32 +351,35 @@ def rank_program(g, core, T, topo):
         tt(A(lw, 16, 32), A(lw, 0, 16), A(n("mb"), 0, 16), OP.mult)
         tt(A(lw, 32, 48), A(lw, 16, 32), A(n("ma"), 0, 16), OP.add)
         turn(A(S, 0, 64), A(du, 0, 64))
-        across(S, "v", "s")
+        more = across(S, 1)
         for h in range(2):
             ts(A(n("th"), 256 * h, 256 * h + 256), A("md%d" % h, 0, 256), A(du, 32 * h, 32 * h + 1), None, OP.mult)
+        more()
+        for h in range(2):
+            tt(A(n("cm"), 256 * h, 256 * h + 256), A(S, 0, 256), A(n("th"), 256 * h, 256 * h + 256), OP.is_gt)
+        rk = n("rk")
+        for h in range(2):
+            o, i, c = A(n("cj"), 256 * h, 256 * h + 256), A(n("cm"), 256 * h, 256 * h + 256), A(rk, h, h + 1)
+            op("s", [o, c], [i], lambda o=o, i=i, c=c: g.scalar.activation(o[4], i[4], AF.Copy, accum_out=c[4]))
         for h in range(2):
             red(A(lw, 48 + h, 49 + h), A(lw, 32 + h, 48, 2), OP.max)
         for h in range(2):
-            tt(A(n("cm"), 256 * h, 256 * h + 256), A(S, 0, 256), A(n("th"), 256 * h, 256 * h + 256), OP.is_gt)
-        for h in range(2):
-            o, i, c = A(n("cj"), 256 * h, 256 * h + 256), A(n("cm"), 256 * h, 256 * h + 256), A(n("rk"), h, h + 1)
-            op("s", [o, c], [i], lambda o=o, i=i, c=c: g.scalar.activation(o[4], i[4], AF.Copy, accum_out=c[4]))
-        for h in range(2):
             ts(A(ev, 8 * h, 8 * h + 8), A(lw, 32 + h, 48, 2), A(lw, 48 + h, 49 + h), None, OP.is_equal)
-        R, rk = n("R"), n("rk")
-        cp("v", A(R, 0, 2), A(rk, 0, 2))
-        cp("v", A(R, 2, 4, 1, 0, 64), A(rk, 0, 2, 1, 64, 128))
-        cp("v", A(R, 2, 4, 1, 64, 128), A(rk, 0, 2, 1, 0, 64))
-        tt(A(ev, 16, 32), A(ev, 0, 16), A("r8", 0, 16), OP.mult)
-        for a in range(4):
+        cp("v", A(rk, 2, 4, 1, 0, 64), A(rk, 0, 2, 1, 64, 128))
+        cp("s", A(rk, 2, 4, 1, 64, 128), A(rk, 0, 2, 1, 0, 64))
+        for a, e in ((0, "v"), (2, "s"), (1, "v"), (3, "s")):
             b = a ^ 1
-            cp("v", A(R, 4, 8, 1, 32 * a, 32 * a + 32), A(R, 0, 4, 1, 32 * b, 32 * b + 32))
-        scatter(A(n("D"), 0, 256), A(R, 0, 8), A("vj", 0, 128))
-        red(A(lw, 50, 51), A(ev, 16, 24), OP.min)
-        gather("v", A(n("dd"), 0, 128), A(n("D"), 0, 64), A("dl", 0, 8))
-        red(A(lw, 51, 52), A(ev, 24, 32), OP.min)
-        for h in range(2):
+            cp(e, A(rk, 4, 8, 1, 32 * a, 32 * a + 32), A(rk, 0, 4, 1, 32 * b, 32 * b + 32))
+        tt(A(ev, 16, 32), A(ev, 0, 16), A("r8", 0, 16), OP.mult)
+        cp("v", A(n("R"), 0, 8), A(rk, 0, 8))
+        scatter(A(n("D"), 0, 256), A(n("R"), 0, 8), A("vj", 0, 128))
+
+        def lost(h):
+            red(A(lw, 50 + h, 51 + h), A(ev, 16 + 8 * h, 24 + 8 * h), OP.min)
             act(A(tl, 32 * h, 32 * h + 32), A("one", 0, 32), AF.Copy, scale=A(lw, 50 + h, 51 + h))
+        lost(0)
+        gather("v", A(n("dd"), 0, 128), A(n("D"), 0, 64), A("dl", 0, 8))
+        lost(1)
         turn(A(n("tt"), 0, 128), A(n("dd"), 0, 128))
         xb, of = n("xb"), n("of")
         tt(A(xb, 0, 4), A(n("tt"), 0, 128, 32), A(n("tt"), 16, 128, 32), OP.add)
@@ -378,15 +388,37 @@ def rank_program(g, core, T, topo):
         deal(t, True)
         deal(t, False)
         turn(A(n("Lz"), 0, 64), A(tl, 0, 64))
-        across(n("Lz"), "v", "s")
+        more = across(n("Lz"), 2 if own != t else 0)
+        v = lambda i: A(n("ol"), 8 * i, 8 * i + 8)
         if own == t:
-            cp("v", A(n("oo"), 0, 1), A(xb, o_, o_ + 1))
-            pick(n("land"), KO * rank, KO * rank + KO, tab, P, A(n("oo"), 0, 1))
-        cp("v", A(n("jf"), 0, 4), A(of, 0, 4))
-        tt(A(n("fr"), 0, 4), A(xb, 0, 4), A(n("jf"), 0, 4), OP.subtract)
-        ts(A(n("op"), 0, 4), A(n("fr"), 0, 4), 1.0 / FR, None, OP.mult)
-        if own == t:
+            even, odd = A(n("qk"), a0, a0 + 16, 2), A(n("qk"), a0 + 1, a0 + 16, 2)
             gather("v", A(n("qk"), 0, 64), A("qn", 0, 256), A(of, 0, 4))
+            cp("v", A(n("oo"), 0, 1), A(xb, o_, o_ + 1))
+            tt(v(0), odd, even, OP.subtract)
+            pick(n("land"), KO * rank, KO * rank + KO, tab, P, A(n("oo"), 0, 1))
+            ts(v(1), v(0), A("oc", 3, 4), None, OP.mult)
+        cp("v", A(n("jf"), 0, 4), A(of, 0, 4))
+        if own == t:
+            tt(v(2), v(1), even, OP.add)
+        tt(A(n("fr"), 0, 4), A(xb, 0, 4), A(n("jf"), 0, 4), OP.subtract)
+        if own == t:
+            ts(v(3), v(2), A("oc", 0, 1), None, OP.is_le)
+            ts(v(4), v(2), A("oc", 2, 3), A("oc", 1, 2), OP.mult, OP.add)
+        ts(A(n("op"), 0, 4), A(n("fr"), 0, 4), 1.0 / FR, None, OP.mult)
+        more()
+        if own == t:
+            tt(v(5), v(3), v(4), OP.add)
+        gather("v", A(n("lk"), 0, 64), A(n("Lz"), 0, 256), A(n("op"), 0, 4))
+        if own == t:
+            ts(v(6), v(5), A("oc", 4, 5), None, OP.add)
+            ts(v(7), v(5), A("oc", 5, 6), None, OP.add)
+            ts(v(8), v(5), KO / 128.0, None, OP.mult)
+            tt(v(10), v(6), A(n("lk"), a0, a0 + 16, 2), OP.is_equal)
+            tt(v(11), v(7), A(n("lk"), a0 + 1, a0 + 16, 2), OP.is_equal)
+            tt(v(9), v(8), A("klc", 0, 8), OP.add)
+            tt(v(12), v(10), v(11), OP.add)
+            tt(v(13), v(12), v(9), OP.add)
+            ts(A(n("oi"), 0, 8), v(13), 128.0, None, OP.mult)
 
     def lists(t):
         n = lambda s: s + str(t)
@@ -395,38 +427,16 @@ def rank_program(g, core, T, topo):
         dma("y", None, A(n("bk"), 0, 64, 1, 0, 1), "st_b%d" % t, 32, out_ap=T.bs[2 * t:2 * t + 1, :])
         dma("y", None, A(n("lr"), 0, 64, 1, 0, 1), "st_b%d" % t, 32, out_ap=T.bs[2 * t + 1:2 * t + 2, :])
 
-    def lostlist(t):
-        n = lambda s: s + str(t)
-        gather("v", A(n("lk"), 0, 64), A(n("Lz"), 0, 256), A(n("op"), 0, 4))
-
     def rebuild(t):
         n = lambda s: s + str(t)
-        ol, a0, qk, lk = n("ol"), KO * o_, n("qk"), n("lk")
-        v = lambda i: A(ol, 8 * i, 8 * i + 8)
-        even = A(qk, a0, a0 + 16, 2)
-        tt(v(0), A(qk, a0 + 1, a0 + 16, 2), even, OP.subtract)
-        ts(v(1), v(0), A("oc", 3, 4), None, OP.mult)
-        tt(v(2), v(1), even, OP.add)
-        ts(v(3), v(2), A("oc", 0, 1), None, OP.is_le)
-        ts(v(4), v(2), A("oc", 2, 3), A("oc", 1, 2), OP.mult, OP.add)
-        tt(v(5), v(3), v(4), OP.add)
-        ts(v(6), v(5), A("oc", 4, 5), None, OP.add)
-        ts(v(7), v(5), A("oc", 5, 6), None, OP.add)
-        ts(v(8), v(5), KO / 128.0, None, OP.mult)
-        tt(v(9), v(8), A("klc", 0, 8), OP.add)
-        lostlist(t)
-        tt(v(10), v(6), A(lk, a0, a0 + 16, 2), OP.is_equal)
-        tt(v(11), v(7), A(lk, a0 + 1, a0 + 16, 2), OP.is_equal)
-        tt(v(12), v(9), v(10), OP.add)
-        tt(v(13), v(12), v(11), OP.add)
-        ts(A(n("oi"), 0, 8), v(13), 128.0, None, OP.mult)
-        tot = 7 * 2 * (full // NO)
-        for r in range(N):
-            if r != rank:
-                for s in ("", "s"):
-                    note([], [A(n("land") + s, KO * r, KO * r + KO)], ("col%d" % t, tot, "remote"))
-        final["col%d" % t] = tot
+        landed([A(n("land") + s, KO * r, KO * r + KO) for r in range(N) if r != rank for s in ("", "s")], "col%d" % t, 7 * 2 * (full // NO))
+        if t == 0:
+            unit(0)
+            unit(1)
         pick(n("ord"), 0, 128, n("land"), 256, A(n("oi"), 0, 8))
+        if t == 0:
+            unit(2)
+            unit(3)
         for b in range(4):
             mm(A("dec", 512 * b, 512 * b + 128), "eq", 128 * b, n("ord"), 0, 128)
         for b in range(4):
@@ -455,28 +465,32 @@ def rank_program(g, core, T, topo):
         scan(A(mmx, 256, 512), A("sd", 0, 256), A(mmx, 0, 256), OP.mult, OP.add)
         cp("v", A(n("ml"), 0, 16), A(mmx, 256 + 15, 512, 16))
 
-    def arrive(t):
-        n = lambda s: s + str(t)
-        others = [o for o in range(NO) if 2 * o + t != rank]
-        tot = len(others) * 2 * full
-        for o in others:
-            for s in ("", "s"):
-                note([], [A(n("W") + s, P + KO * o, P + KO * o + KO)], ("new%d" % t, tot, "remote"))
-        final["new%d" % t] = tot
-
     def finish(t):
-        cp("s", A("M%d" % t, 0, 384), A("nat", 0, 384))
+        n = lambda s: s + str(t)
         if own == t:
             rebuild(t)
-        else:
-            lostlist(t)
+        if t == 0:
+            act(A("xa", 0, 256), A("x16", 0, 256), AF.Abs, bias=A("ng", 1, 2))
+            act(A("mk", 0, 256), A("xa", 0, 256), AF.Relu, bias=1.0, scale=-1.0)
+            act(A("sd", 0, 256), A("x16", 0, 256), AF.Sign)
+            ts(A("dkw", 0, 4), A("dk", 0, 4), A("fb", 3, 4), None, OP.add)
+        cp("s", A(n("M"), 0, P), A("nat", 0, P))
         lists(t)
         newlist(t)
-        arrive(t)
+        if t == 0:
+            quant("W0", 0, 256, "tbt", 0)
+            ts(A("ma1", 0, 16), A("rc", 0, 16), A("fb", 1, 2), -1.0, OP.is_equal, OP.mult)
+            ts(A("mb1", 0, 16), A("rc", 0, 16), A("fb", 1, 2), None, OP.not_equal)
+            act(A("D1", 0, 256), A("nat", 0, 256), AF.Copy, scale=0.0)
+            if own:
+                owner()
+                for b in range(4):
+                    unit(b)
+        others = [o for o in range(NO) if 2 * o + t != rank]
+        landed([A(n("W") + s, P + KO * o, P + KO * o + KO) for o in others for s in ("", "s")], "new%d" % t, len(others) * 2 * full)
 
     judge(0, "tA")
     finish(0)
-    act(A("D1", 0, 256), A("nat", 0, 256), AF.Copy, scale=0.0)
     checks(1, "tB", lambda h: pick("tB", 128 * h, 128 * h + 128, "W0", P + K, A("ml0", 8 * h, 8 * h + 8)))
     pick("W1", 0, P, "W0", P + K, A("ml0", 0, 16))
     quant("wq", 0, 128, "wt", 0)
@@ -485,9 +499,10 @@ def rank_program(g, core, T, topo):
     for h in range(2):
         pick("F", 128 * h, 128 * h + 128, "W1", P + K, A("ml1", 8 * h, 8 * h + 8))
         mm(A("py", 512 * h, 512 * h + 128), "wq", 0, "F", 128 * h, 128 * h + 128)
-    cp("s", A("yb", 0, 128), A("py", 0, 128))
-    cp("v", A("yb", 128, 256), A("py", 512, 640))
-    dma("y", None, A("F", 0, P), "st_c", 16, out_ap=T.oc[:], in_ap=T.F[:, 0:P].bitcast(dt.uint8))
+        dma("y", None, A("F", 128 * h, 128 * h + 128), "st_c", 32, out_ap=T.oc[:, 512 * h:512 * h + 512],
+            in_ap=T.F[:, 128 * h:128 * h + 128].bitcast(dt.uint8))
+    cp("v", A("yb", 0, 128), A("py", 0, 128))
+    cp("s", A("yb", 128, 256), A("py", 512, 640))
     dma("y", None, A("yb", 0, 128), "st_y", 32, out_ap=T.y[:, 0:128])
     dma("s", None, A("yb", 128, 256), "st_y", 32, out_ap=T.y[:, 128:256])
     for k in range(4):

@@ -5,6 +5,7 @@ OP = AluOpType
 AF = ActivationFunctionType
 X = AxisListType.X
 N, P, K, NO, KO = 8, 256, 64, 4, 16
+BIG = 1e29
 STEP = 1.0 - 2.0 ** -24
 TINY = 2.0 ** -118
 FR = 2.0 ** -10
@@ -33,25 +34,28 @@ def _parts(buf, *parts):
 
 for _n, _w in (("tbt", 4 * P), ("ut", 512), ("wt", 512), ("ee", 528), ("zt", 512)):
     _sb(_n, _w, "bfloat16")
-_parts("con", ("rc", 16), ("r8", 16), ("jc", 2), ("ad", 4), ("ad2", 4), ("hb", 64), ("hx", 32), ("hp", 32), ("hq", 32), ("hr", 32),
-       ("kl0", 8), ("dk", 4), ("dl0", 8), ("fb", 5), ("sd16", 16), ("one", 32), ("oc", 8), ("klc", 8),
-       ("dkw", 4), ("ng", 4), ("ae", 4), ("ma0", 16), ("ma1", 16), ("mb0", 16), ("mb1", 16))
-for _n, _w in (("nat", 528), ("ea", 528), ("x16", 256), ("xa", 256), ("q8", 264), ("qn", 256), ("jp", 256), ("md0", 256), ("md1", 256),
-               ("vj", 128), ("mk", 256), ("sd", 256), ("dpat", 128), ("yb", 256)):
+_parts("con", ("rc", 32), ("hm", 32), ("jc", 1), ("ad", 4), ("ad2", 4), ("hb", 128), ("hx", 32), ("hp", 32), ("hq", 32), ("hr", 32),
+       ("kl0", 8), ("dl0", 8), ("fb", 5), ("fc", 3), ("u1", 2), ("sd32", 32), ("sp", 16), ("one", 32), ("oc", 8), ("klc", 8),
+       ("ng", 4), ("ae", 4), ("eq0", 32), ("eq1", 32), ("dm0", 32), ("dm1", 32), ("gm0", 16), ("gm1", 16), ("lof", 4))
+for _n, _w in (("nat", 528), ("ea", 528), ("x16", 272), ("xa0", 256), ("xa1", 256), ("xm0", 256), ("xm1", 256), ("q8", 264), ("qn", 256),
+               ("jp", 128), ("md", 132), ("vj", 128), ("sd", 256), ("dpat", 128), ("yb", 256)):
     _sb(_n, _w)
 _sb("pi", 2, "int32")
 _sb("ib", 5, "int32")
+_sb("id", 3, "int32")
 _sb("cl", 2, "uint16")
+_sb("lo", 4, "uint16")
 _sb("dl", 8, "uint16")
 for _n, _w in (("tA", P), ("tB", P), ("F", P), ("uq", 128), ("wq", 128), ("eq", 512)):
     _mx(_n, _w)
 for _t in "01":
-    _parts("jd" + _t, ("d1" + _t, 32), ("so" + _t, 32), ("du" + _t, 64), ("lw" + _t, 64), ("ev" + _t, 32), ("tl" + _t, 64), ("rk" + _t, 8), ("tt" + _t, 128),
-           ("xb" + _t, 4), ("jf" + _t, 4), ("fr" + _t, 4), ("ol" + _t, 128), ("w" + _t, 160), ("th" + _t, 512), ("cm" + _t, 512),
-           ("cj" + _t, 512), ("mm" + _t, 512))
-    for _n, _w in (("L", 32), ("S", 256), ("Lz", 256), ("D", 256), ("dd", 128), ("bk", 64), ("lk", 64), ("lr", 64), ("qk", 64), ("M", 384)):
+    _parts("jd" + _t, ("d1" + _t, 32), ("so" + _t, 32), ("du" + _t, 64), ("lw" + _t, 32), ("px" + _t, 16), ("tl" + _t, 64), ("rk" + _t, 4),
+           ("tt" + _t, 128), ("xb" + _t, 4), ("jf" + _t, 4), ("fr" + _t, 4), ("ol" + _t, 128), ("wg" + _t, 64), ("wa" + _t, 64),
+           ("wb" + _t, 64), ("wc" + _t, 64), ("wd" + _t, 64), ("we" + _t, 64), ("wf" + _t, 64), ("th" + _t, 264), ("cm" + _t, 260),
+           ("ca" + _t, 2), ("cb" + _t, 2), ("ls" + _t, 2), ("rl" + _t, 256), ("cj" + _t, 256), ("lj" + _t, 16), ("mm" + _t, 256))
+    for _n, _w in (("L", 32), ("S", 256), ("Lz", 256), ("D", 256), ("dd", 128), ("bk", 64), ("lk", 64), ("lr", 64), ("qk", 64), ("M", 256)):
         _sb(_n + _t, _w)
-    for _n, _w in (("R", 8), ("of", 4), ("op", 4), ("oo", 2), ("mo", 4), ("ml", 16), ("oi", 8)):
+    for _n, _w in (("R", 8), ("of", 4), ("op", 4), ("oo", 2), ("ml", 16), ("oi", 8)):
         _sb(_n + _t, _w, "uint16")
     _sb("h" + _t, 512, "bfloat16")
     for _n, _w in (("slot", K), ("land", 256), ("ord", 128), ("new", 128), ("W", P + K)):
@@ -62,7 +66,7 @@ SCRATCH["py"] = ("psum", [128, 1024], "float32")
 PSUM = ("pc", "dec", "py")
 
 SEMAPHORES = ["qv", "qs", "qt", "qg", "out", "ld_u", "ld_a", "ld_b", "ld_w", "st_c", "st_s", "st_y",
-              "st_b0", "st_b1", "ck0", "ck1", "col0", "col1", "new0", "new1"]
+              "st_b0", "st_b1", "ck0", "ck1", "col0", "col0s", "col1", "col1s", "new0", "new0s", "new1", "new1s"]
 
 
 def rank_program(g, core, T, topo):
@@ -137,14 +141,16 @@ def rank_program(g, core, T, topo):
         else:
             op("v", [out], ins, lambda: g.vector.tensor_scalar(out[4], a[4], v1, v2, o0, o1))
 
-    def act(out, a, f, bias=None, scale=None):
+    def act(out, a, f, bias=None, scale=None, total=None):
         ins = [a] + [s for s in (bias, scale) if isinstance(s, tuple)]
         kw = {}
         if bias is not None:
             kw["bias"] = bias[4] if isinstance(bias, tuple) else bias
         if scale is not None:
             kw["scale"] = scale[4] if isinstance(scale, tuple) else scale
-        op("s", [out], ins, lambda: g.scalar.activation(out[4], a[4], f, **kw))
+        if total is not None:
+            kw["accum_out"] = total[4]
+        op("s", [out] if total is None else [out, total], ins, lambda: g.scalar.activation(out[4], a[4], f, **kw))
 
     def cp(e, out, a):
         if e == "v":
@@ -155,38 +161,48 @@ def rank_program(g, core, T, topo):
     def fill(out, x):
         op("v", [out], [], lambda: g.vector.memset(out[4], x))
 
+    def const(out, x, like):
+        act(out, like, AF.Identity, bias=x, scale=0.0)
+
     def red(out, a, o):
         op("v", [out], [a], lambda: g.vector.tensor_reduce(out[4], a[4], X, o))
 
-    def scan(out, d0, d1, o0, o1):
-        op("v", [out], [d0, d1], lambda: g.vector.tensor_tensor_scan(out[4], d0[4], d1[4], 0.0, o0, o1))
+    def scan(out, d0, d1, o0, o1, first=None):
+        op("v", [out], [d0, d1] + ([first] if first else []),
+           lambda: g.vector.tensor_tensor_scan(out[4], d0[4], d1[4], first[4] if first else 0.0, o0, o1))
 
     def turn(out, a):
         op("v", [out], [a], lambda: g.vector.transpose(out[4], a[4]))
 
-    part = [False]
-
     def iota(out, pat, base, cm, flag=True):
         kw = {"allow_small_or_imprecise_dtypes": True} if flag else {}
-        now = out[1] != 0 or out[2] != 128
-        if now or part[0]:
-            wait("g", "qg", count["g"])
-        part[0] = now
         op("g", [out], [], lambda: g.iota(out[4], pat, base, cm, **kw))
 
-    def gather(e, out, win, off):
+    def gather(e, out, win, off, f=AF.Copy):
         if e == "v":
             op("v", [out], [win, off], lambda: g.vector.tensor_copy(out[4], win[4].indirect(off[4])))
         else:
-            op("s", [out], [win, off], lambda: g.scalar.activation(out[4], win[4].indirect(off[4]), AF.Copy))
+            op("s", [out], [win, off], lambda: g.scalar.activation(out[4], win[4].indirect(off[4]), f))
 
     def scatter(win, off, val):
         op("v", [win], [val, off], lambda: g.vector.tensor_copy(win[4].indirect(off[4]), val[4]))
 
-    def pick(dst, c0, c1, src, n, off):
+    def pickc(dst, c0, c1, src, n, off):
         o, i = A(dst, c0, c1), A(src, 0, n)
         op("v", [o], [i, off], lambda: g.vector.tensor_copy(o[4].bitcast(dt.uint32), i[4].bitcast(dt.uint32).indirect(off[4])))
-        gather("s", A(dst + "s", c0, c1), A(src + "s", 0, n), off)
+
+    def picks(e, dst, c0, c1, src, n, off):
+        gather(e, A(dst + "s", c0, c1), A(src + "s", 0, n), off)
+
+    def pick(dst, c0, c1, src, n, off):
+        pickc(dst, c0, c1, src, n, off)
+        picks("s", dst, c0, c1, src, n, off)
+
+    def pick2(dst, n1, src, n, off, k):
+        for h in range(2):
+            pickc(dst, n1 * h, n1 * h + n1, src, n, A(off, k * h, k * h + k))
+        for h, e in ((0, "s"), (1, "v")):
+            picks(e, dst, n1 * h, n1 * h + n1, src, n, A(off, k * h, k * h + k))
 
     def quant(dst, c0, c1, tile, at):
         o, s, i = A(dst, c0, c1), A(dst + "s", c0, c1), A(tile, at, at + 4 * (c1 - c0))
@@ -234,7 +250,7 @@ def rank_program(g, core, T, topo):
             order("g", [src], [])
             d = A("land%d" % t + s, KO * rank, KO * rank + KO)
             tr.append(RemoteDMATransfer(dst_ids=[dest(c)], dma_engine_mask=sum(1 << e for e in es[w * o:w * o + w]),
-                                        remote_sem=T.sem["col%d" % t], srcs=[raw(src, codes)], dsts=[raw(d, codes)]))
+                                        remote_sem=T.sem["col%d" % t + s], srcs=[raw(src, codes)], dsts=[raw(d, codes)]))
             final["out"] = final.get("out", 0) + w
         g.remote_dma_fused(tr, local_sem=T.sem["out"])
 
@@ -249,83 +265,114 @@ def rank_program(g, core, T, topo):
     dma("y", A("wt", 0, 512), None, "ld_w", 16, in_ap=T.w[:])
 
     iota(A("pi", 0, 2), [[1, 2]], 0, 1, False)
-    iota(A("rc", 0, 16), [[1, 8], [0, 2]], 0, 0)
     iota(A("nat", 0, 128), [[1, 128]], 0, 0)
-    iota(A("jc", 0, 2), [[128, 2]], 0, 1)
-    iota(A("hb", 0, 64), [[128, 2], [1, 32]], 0, 0)
-    iota(A("hx", 0, 32), [[128, 2], [1, 16]], 0, 0)
-    iota(A("hp", 0, 32), [[32, 2], [1, 16]], 0, 0)
-    iota(A("r8", 0, 16), [[0, 2], [1, 8]], -8, 0)
-    iota(A("dl0", 0, 8), [[16, 4], [0, 2]], 0, 0)
-    for a in range(4):
-        iota(A("ad", 0, 4, 1, 32 * a, 32 * a + 32), [[32 * ((a ^ 1) - a), 2], [32 * ((a ^ 2) - a), 2]], 32 * a, 0)
+    iota(A("rc", 0, 32), [[0, 4], [1, 8]], 0, 0)
+    iota(A("hm", 0, 32), [[0, 2], [1, 2], [0, 8]], 0, 0)
+    iota(A("jc", 0, 1), [[1, 1]], 0, 1)
     fill(A("ut", 8, 512), 0.0)
     fill(A("one", 0, 32), 1.0)
-    fill(A("sd16", 1, 16), 1.0)
-    fill(A("sd16", 0, 1), 0.0)
     for col, (src, bits) in enumerate(((0, 7), (1, 7), (0, 16), (0, 15), (0, 8))):
         ts(A("ib", col, col + 1), A("pi", src, src + 1), bits, None, OP.bitwise_and)
     cp("v", A("fb", 0, 5), A("ib", 0, 5))
-    ts(A("ma0", 0, 16), A("rc", 0, 16), A("fb", 0, 1), -1.0, OP.is_equal, OP.mult)
-    ts(A("mb0", 0, 16), A("rc", 0, 16), A("fb", 0, 1), None, OP.not_equal)
-    ts(A("ng", 0, 1), A("jc", 0, 1), -4.0, -4.0, OP.mult, OP.add)
-    ts(A("ng", 1, 2), A("fb", 3, 4), -1.0, None, OP.mult)
+
+    def masks(t):
+        n = str(t)
+        ts(A("eq" + n, 0, 32), A("rc", 0, 32), A("fb", t, t + 1), -1.0, OP.is_equal, OP.mult)
+        ts(A("gm" + n, 0, 16), A("rc", 0, 16), A("fb", t, t + 1), BIG, OP.is_equal, OP.mult)
+        tt(A("dm" + n, 0, 32), A("eq" + n, 0, 32), A("hm", 0, 32), OP.add)
+
+    masks(0)
     quant("uq", 0, 128, "ut", 0)
     act(A("nat", 128, 256), A("nat", 0, 128), AF.Identity, bias=128.0)
     act(A("nat", 256, 512), A("nat", 0, 256), AF.Identity, bias=256.0)
     act(A("nat", 512, 528), A("nat", 0, 16), AF.Identity, bias=512.0)
-    act(A("D0", 0, 256), A("nat", 0, 256), AF.Copy, scale=0.0)
+    act(A("ng", 0, 1), A("jc", 0, 1), AF.Identity, bias=-4.0, scale=-4.0)
+    act(A("ea", 0, 528), A("nat", 0, 528), AF.Abs, bias=A("ng", 0, 1))
+    act(A("ee", 0, 528), A("ea", 0, 528), AF.Relu, bias=1.0, scale=-1.0)
 
-    def checks(t, tab, half):
+    def checks(t, tab, half, e0):
         for h in range(2):
             half(h)
             mm(A("pc", 512 * h, 512 * h + 128), tab, 128 * h, "uq", 0, 128)
-        for h, e in ((0, "s"), (1, "v")):
+        for h, e in ((0, e0), (1, "v")):
             cp(e, A("L%d" % t, 4 * rank + 2 * h, 4 * rank + 2 * h + 2), A("pc", 512 * h, 512 * h + 2))
         spread(A("L%d" % t, 4 * rank, 4 * rank + 4), "ck%d" % t)
         landed([A("L%d" % t, 4 * r, 4 * r + 4) for r in range(N) if r != rank], "ck%d" % t, 7 * full)
 
-    checks(0, "tA", lambda h: quant("tA", 128 * h, 128 * h + 128, "tbt", 512 * h))
+    checks(0, "tA", lambda h: quant("tA", 128 * h, 128 * h + 128, "tbt", 512 * h), "v")
 
+    iota(A("hb", 0, 128), [[0, 4], [1, 32]], 0, 0)
+    iota(A("hx", 0, 32), [[128, 2], [1, 16]], 0, 0)
+    iota(A("hp", 0, 32), [[32, 2], [1, 16]], 0, 0)
+    iota(A("dl0", 0, 8), [[16, 4], [0, 2]], 0, 0)
+    iota(A("x16", 0, 272), [[0, 17], [1, 16]], 0, 0)
+    iota(A("q8", 0, 264), [[0, 33], [1, 8]], 0, 0)
+    iota(A("kl0", 0, 8), [[2, 8]], 0, 0)
+    for col, bits in enumerate((96, 64, 32)):
+        ts(A("id", col, col + 1), A("pi", 0, 1), bits, None, OP.bitwise_and)
+    cp("v", A("fc", 0, 3), A("id", 0, 3))
+    ts(A("lo", 0, 1), A("fb", 0, 1), 4.0, None, OP.mult)
+    ts(A("lo", 1, 2), A("fb", 0, 1), 4.0, 2.0, OP.mult, OP.add)
+    cp("s", A("ad", 0, 1), A("fc", 0, 1))
+    act(A("u1", 0, 1), A("fc", 1, 2), AF.Identity, bias=64.0, scale=-1.0)
+    act(A("u1", 1, 2), A("fc", 2, 3), AF.Identity, bias=32.0, scale=-1.0)
+    act(A("ad", 3, 4), A("fc", 0, 1), AF.Identity, bias=96.0, scale=-1.0)
+    act(A("ad", 1, 2), A("u1", 0, 1), AF.Identity, bias=A("fc", 2, 3))
+    act(A("ad", 2, 3), A("u1", 1, 2), AF.Identity, bias=A("fc", 1, 2))
     for s in range(4):
-        ts(A("jp", 64 * s, 64 * s + 64), A("hb", 0, 64), A("ad", s, s + 1), None, OP.add)
-    ts(A("ad2", 0, 1), A("fb", 2, 3), 1.0 + FR, None, OP.mult)
-    ts(A("hq", 0, 32), A("hp", 0, 32), FR, None, OP.mult)
-    for h in range(2):
-        ts(A("md%d" % h, 0, 256), A("jp", 0, 256), A("jc", h, h + 1), STEP, OP.is_ge, OP.max)
+        act(A("jp", 32 * s, 32 * s + 32), A("hb", 32 * s, 32 * s + 32), AF.Identity, bias=A("ad", s, s + 1))
+    act(A("lof", 0, 1), A("fb", 4, 5), AF.Identity, bias=1.0, scale=0.25)
+    act(A("lof", 1, 2), A("fb", 0, 1), AF.Identity, bias=A("lof", 0, 1), scale=4.0)
+    act(A("ad2", 0, 1), A("fb", 2, 3), AF.Copy, scale=1.0 + FR)
+    act(A("hq", 0, 32), A("hp", 0, 32), AF.Copy, scale=FR)
+    act(A("ae", 0, 4), A("ad", 0, 4), AF.Identity, bias=A("ad2", 0, 1))
+    const(A("md", 128, 129), -1.0, A("nat", 0, 1))
+    cp("s", A("sd32", 0, 32), A("one", 0, 32))
+    const(A("sd32", 0, 32, 16), 0.0, A("nat", 0, 2))
+    for t in "01":
+        const(A("cm" + t, 256, 257), 128.0, A("nat", 0, 1))
+    const(A("sp", 0, 16), 0.0, A("nat", 0, 16))
+    const(A("sp", 0, 16, 8), -BIG, A("nat", 0, 2))
+    const(A("D0", 0, 256), 0.0, A("nat", 0, 256))
+
+    def owner():
+        cp("s", A("qn", 0, 256), A("q8", own, own + 256))
+        act(A("oc", 3, 4), A("fb", 4, 5), AF.Copy, scale=0.125)
+        act(A("oc", 0, 1), A("fb", 0, 1), AF.Identity, bias=-1.0)
+        act(A("oc", 1, 2), A("fb", 0, 1), AF.Relu, bias=-1.0)
+        act(A("oc", 2, 3), A("fb", 0, 1), AF.Relu, bias=1.0, scale=-1.0)
+        act(A("oc", 4, 5), A("fb", 4, 5), AF.Identity, bias=-8.0, scale=12.5)
+        act(A("oc", 5, 6), A("fb", 4, 5), AF.Identity, bias=92.0, scale=-12.5)
+        act(A("oc", 6, 7), A("fb", 4, 5), AF.Copy, scale=0.125 / 128)
+        act(A("klc", 0, 8), A("kl0", 0, 8), AF.Identity, bias=A("oc", 6, 7), scale=1.0 / 128)
+
+    def owner_v():
+        fill(A("zt", 0, 512), 0.0)
+        fill(A("dpat", 0, 128), 1.0)
+        ts(A("cl", 0, 1), A("fb", 3, 4), 8.0, 7.0, OP.mult, OP.add)
+        fill(A("dpat", 0, 128, 8), 0.0)
+        fill(A("dpat", 1, 128, 8), -1.0)
+        quant("land%d" % own, 128, 256, "zt", 0)
+        for b in range(4):
+            quant("eq", 128 * b, 128 * b + 128, "ee", 4 - b)
+
+    quant("W0", 0, 256, "tbt", 0)
+    if own == 0:
+        owner_v()
+    cp("v", A("lo", 2, 3), A("lof", 1, 2))
+    ts(A("md", 0, 128), A("jp", 0, 128), A("jc", 0, 1), STEP, OP.is_ge, OP.max)
     tt(A("hr", 0, 32), A("hq", 0, 32), A("hx", 0, 32), OP.add)
-    ts(A("ae", 0, 4), A("ad", 0, 4), A("ad2", 0, 1), None, OP.add)
     for s in range(4):
         ts(A("vj", 32 * s, 32 * s + 32), A("hr", 0, 32), A("ae", s, s + 1), 64.0 * FR * s, OP.add, OP.add)
     ts(A("dl", 0, 8), A("dl0", 0, 8), A("fb", 3, 4), None, OP.add)
-    iota(A("q8", 0, 264), [[0, 33], [1, 8]], 0, 0)
-    iota(A("kl0", 0, 8), [[2, 8]], 0, 0)
-    iota(A("x16", 0, 256), [[0, 16], [1, 16]], 0, 0)
-    iota(A("dk", 0, 4), [[16, 4]], P + K, 0)
-    act(A("ea", 0, 528), A("nat", 0, 528), AF.Abs, bias=A("ng", 0, 1))
-    act(A("ee", 0, 528), A("ea", 0, 528), AF.Relu, bias=1.0, scale=-1.0)
-    act(A("zt", 0, 512), A("nat", 0, 512), AF.Copy, scale=0.0)
-    cp("s", A("qn", 0, 256), A("q8", own, own + 256))
 
-    def owner():
-        fill(A("dpat", 0, 128), 1.0)
-        ts(A("oc", 0, 1), A("fb", 0, 1), -1.0, None, OP.add)
-        ts(A("oc", 1, 2), A("fb", 0, 1), -1.0, 0.0, OP.add, OP.max)
-        ts(A("oc", 2, 3), A("fb", 0, 1), 0.0, None, OP.is_equal)
-        fill(A("dpat", 0, 128, 8), 0.0)
-        fill(A("dpat", 1, 128, 8), -1.0)
-        ts(A("oc", 3, 4), A("fb", 4, 5), 0.125, None, OP.mult)
-        ts(A("oc", 4, 5), A("fb", 4, 5), 12.5, -8.0, OP.mult, OP.add)
-        ts(A("oc", 5, 6), A("fb", 4, 5), -12.5, 92.0, OP.mult, OP.add)
-        ts(A("cl", 0, 1), A("fb", 3, 4), 8.0, 7.0, OP.mult, OP.add)
-        ts(A("klc", 0, 8), A("kl0", 0, 8), A("oc", 3, 4), 1.0 / 128, OP.add, OP.mult)
-        quant("land%d" % own, 128, 256, "zt", 0)
+    def shift(t):
+        return rank if t == 0 else -rank % P
 
-    def unit(b):
-        quant("eq", 128 * b, 128 * b + 128, "ee", 4 - b)
-
-    if own == 0:
-        owner()
+    def lanes(t):
+        n, c = str(t), -shift(t) % 16
+        act(A("xa" + n, 0, 256), A("x16", c, c + 256), AF.Abs, bias=A("ng", 1, 2))
+        act(A("xm" + n, 0, 256), A("xa" + n, 0, 256), AF.Relu, bias=1.0, scale=-1.0)
 
     def across(buf, v):
         cp("v", A(buf, 64, 128, 1, 0, 64), A(buf, 0, 64, 1, 64, 128))
@@ -338,48 +385,52 @@ def rank_program(g, core, T, topo):
         rest("s", v, 4)
         return lambda: rest("v", 0, v)
 
-    def judge(t, tab):
+    def judge(t, tab, meanwhile):
         n = lambda s: s + str(t)
-        L, d1, so, du, S, lw, ev, tl = n("L"), n("d1"), n("so"), n("du"), n("S"), n("lw"), n("ev"), n("tl")
-        act(A(lw, 0, 16), A(L, 1, 32, 2), AF.Abs)
-        tt(A(d1, 0, 16), A(L, 0, 32, 2), A(n("ma"), 0, 16), OP.mult)
-        tt(A(d1, 16, 32), A(L, 0, 32, 2), A(n("mb"), 0, 16), OP.mult)
-        for h in range(2):
-            scan(A(so, 16 * h, 16 * h + 16), A("sd16", 0, 16), A(d1, h, 32, 2), OP.mult, OP.subtract)
+        L, d1, so, du, S, lw, px, tl = n("L"), n("d1"), n("so"), n("du"), n("S"), n("lw"), n("px"), n("tl")
+        th, cm, cj, rl, ca, cb, ls, rk, R = n("th"), n("cm"), n("cj"), n("rl"), n("ca"), n("cb"), n("ls"), n("rk"), n("R")
+        o, i, f, m = A(d1, 0, 32), A(L, 0, 32), A("lo", 0, 2), A(n("dm"), 0, 32)
+        op("v", [o], [i, f, m], lambda: g.vector.tensor_tensor(o[4], i[4].indirect(f[4]), m[4], OP.mult))
+        gather("s", A(lw, 0, 16), i, A("lo", 2, 3), AF.Abs)
+        scan(A(so, 0, 32), A("sd32", 0, 32), A(d1, 0, 32), OP.mult, OP.subtract)
         for h in range(2):
             act(A(du, 32 * h, 32 * h + 32), A("one", 0, 32), AF.Abs, bias=TINY, scale=A(so, 16 * h + 15, 16 * h + 16))
-        tt(A(lw, 16, 32), A(lw, 0, 16), A(n("mb"), 0, 16), OP.mult)
-        tt(A(lw, 32, 48), A(lw, 16, 32), A(n("ma"), 0, 16), OP.add)
-        turn(A(S, 0, 64), A(du, 0, 64))
-        more = across(S, 1)
         for h in range(2):
-            ts(A(n("th"), 256 * h, 256 * h + 256), A("md%d" % h, 0, 256), A(du, 32 * h, 32 * h + 1), None, OP.mult)
-        more()
+            act(A(th, 132 * h, 132 * h + 129), A("md", 0, 129), AF.Copy, scale=A(du, 32 * h, 32 * h + 1))
+        tt(A(lw, 16, 32), A(lw, 0, 16), A(n("gm"), 0, 16), OP.subtract)
+        scan(A(px, 0, 16), A("sp", 0, 16), A(lw, 16, 32), OP.add, OP.max)
         for h in range(2):
-            tt(A(n("cm"), 256 * h, 256 * h + 256), A(S, 0, 256), A(n("th"), 256 * h, 256 * h + 256), OP.is_gt)
-        rk = n("rk")
+            turn(A(S, 128 * h, 128 * h + 32), A(du, 32 * h, 32 * h + 32))
+        for h in (0, 128):
+            cp("v", A(S, h + 32, h + 64, 1, 0, 64), A(S, h, h + 32, 1, 64, 128))
+            cp("s", A(S, h + 32, h + 64, 1, 64, 128), A(S, h, h + 32, 1, 0, 64))
+        for h in (0, 128):
+            for a, e in ((0, "v"), (2, "s"), (1, "v"), (3, "s")):
+                b = a ^ 1
+                cp(e, A(S, h + 64, h + 128, 1, 32 * a, 32 * a + 32), A(S, h, h + 64, 1, 32 * b, 32 * b + 32))
+        act(A(rl, 0, 128), A(S, 128, 256), AF.Relu, bias=A(th, 128, 129))
+        act(A(rl, 128, 256), A(S, 0, 128), AF.Relu, bias=A(du, 32, 33), scale=-1.0)
+        act(A(cj, 0, 128), A(rl, 0, 128), AF.Sign, total=A(ca, 0, 1))
+        act(A(cj, 128, 256), A(rl, 128, 256), AF.Sign, scale=-1.0, total=A(ca, 1, 2))
         for h in range(2):
-            o, i, c = A(n("cj"), 256 * h, 256 * h + 256), A(n("cm"), 256 * h, 256 * h + 256), A(rk, h, h + 1)
-            op("s", [o, c], [i], lambda o=o, i=i, c=c: g.scalar.activation(o[4], i[4], AF.Copy, accum_out=c[4]))
+            act(A(n("lj"), 8 * h, 8 * h + 8), A(px, 8 * h, 8 * h + 8), AF.Sign, bias=A(px, 8 * h + 7, 8 * h + 8), scale=-1.0,
+                total=A(ls, h, h + 1))
         for h in range(2):
-            red(A(lw, 48 + h, 49 + h), A(lw, 32 + h, 48, 2), OP.max)
+            act(A(tl, 32 * h, 32 * h + 32), A("one", 0, 32), AF.Identity, bias=-8.0, scale=A(ls, h, h + 1))
+        meanwhile()
         for h in range(2):
-            ts(A(ev, 8 * h, 8 * h + 8), A(lw, 32 + h, 48, 2), A(lw, 48 + h, 49 + h), None, OP.is_equal)
-        cp("v", A(rk, 2, 4, 1, 0, 64), A(rk, 0, 2, 1, 64, 128))
-        cp("s", A(rk, 2, 4, 1, 64, 128), A(rk, 0, 2, 1, 0, 64))
-        for a, e in ((0, "v"), (2, "s"), (1, "v"), (3, "s")):
+            tt(A(cm, 128 * h, 128 * h + 128), A(S, 128 * h, 128 * h + 128), A(th, 132 * h, 132 * h + 128), OP.is_gt)
+        red(A(cb, 0, 1), A(cm, 0, 128), OP.add)
+        red(A(cb, 1, 2), A(cm, 128, 257), OP.add)
+        tt(A(rk, 0, 2), A(ca, 0, 2), A(cb, 0, 2), OP.add)
+        tt(A(rk, 2, 4, 1, 0, 64), A(ca, 0, 2, 1, 64, 128), A(cb, 0, 2, 1, 64, 128), OP.add)
+        tt(A(rk, 2, 4, 1, 64, 128), A(ca, 0, 2, 1, 0, 64), A(cb, 0, 2, 1, 0, 64), OP.add)
+        cp("v", A(R, 0, 4), A(rk, 0, 4))
+        for a in range(4):
             b = a ^ 1
-            cp(e, A(rk, 4, 8, 1, 32 * a, 32 * a + 32), A(rk, 0, 4, 1, 32 * b, 32 * b + 32))
-        tt(A(ev, 16, 32), A(ev, 0, 16), A("r8", 0, 16), OP.mult)
-        cp("v", A(n("R"), 0, 8), A(rk, 0, 8))
-        scatter(A(n("D"), 0, 256), A(n("R"), 0, 8), A("vj", 0, 128))
-
-        def lost(h):
-            red(A(lw, 50 + h, 51 + h), A(ev, 16 + 8 * h, 24 + 8 * h), OP.min)
-            act(A(tl, 32 * h, 32 * h + 32), A("one", 0, 32), AF.Copy, scale=A(lw, 50 + h, 51 + h))
-        lost(0)
+            cp("v", A(R, 4, 8, 1, 32 * a, 32 * a + 32), A(rk, 0, 4, 1, 32 * b, 32 * b + 32))
+        scatter(A(n("D"), 0, 256), A(R, 0, 8), A("vj", 0, 128))
         gather("v", A(n("dd"), 0, 128), A(n("D"), 0, 64), A("dl", 0, 8))
-        lost(1)
         turn(A(n("tt"), 0, 128), A(n("dd"), 0, 128))
         xb, of = n("xb"), n("of")
         tt(A(xb, 0, 4), A(n("tt"), 0, 128, 32), A(n("tt"), 16, 128, 32), OP.add)
@@ -410,9 +461,9 @@ def rank_program(g, core, T, topo):
             tt(v(5), v(3), v(4), OP.add)
         gather("v", A(n("lk"), 0, 64), A(n("Lz"), 0, 256), A(n("op"), 0, 4))
         if own == t:
-            ts(v(6), v(5), A("oc", 4, 5), None, OP.add)
-            ts(v(7), v(5), A("oc", 5, 6), None, OP.add)
-            ts(v(8), v(5), KO / 128.0, None, OP.mult)
+            act(v(6), v(5), AF.Identity, bias=A("oc", 4, 5))
+            act(v(7), v(5), AF.Identity, bias=A("oc", 5, 6))
+            act(v(8), v(5), AF.Copy, scale=KO / 128.0)
             tt(v(10), v(6), A(n("lk"), a0, a0 + 16, 2), OP.is_equal)
             tt(v(11), v(7), A(n("lk"), a0 + 1, a0 + 16, 2), OP.is_equal)
             tt(v(9), v(8), A("klc", 0, 8), OP.add)
@@ -429,14 +480,9 @@ def rank_program(g, core, T, topo):
 
     def rebuild(t):
         n = lambda s: s + str(t)
-        landed([A(n("land") + s, KO * r, KO * r + KO) for r in range(N) if r != rank for s in ("", "s")], "col%d" % t, 7 * 2 * (full // NO))
-        if t == 0:
-            unit(0)
-            unit(1)
-        pick(n("ord"), 0, 128, n("land"), 256, A(n("oi"), 0, 8))
-        if t == 0:
-            unit(2)
-            unit(3)
+        for s in ("", "s"):
+            landed([A(n("land") + s, KO * r, KO * r + KO) for r in range(N) if r != rank], "col%d" % t + s, 7 * (full // NO))
+        pick2(n("ord"), 64, n("land"), 256, n("oi"), 4)
         for b in range(4):
             mm(A("dec", 512 * b, 512 * b + 128), "eq", 128 * b, n("ord"), 0, 128)
         for b in range(4):
@@ -444,68 +490,69 @@ def rank_program(g, core, T, topo):
         quant(n("new"), 0, 128, n("h"), 0)
         pick(n("W"), P + a0, P + a0 + KO, n("new"), 128, A("cl", 0, 1))
         spread(A(n("W"), P + a0, P + a0 + KO), "new%d" % t, True)
-        spread(A(n("W") + "s", P + a0, P + a0 + KO), "new%d" % t)
+        spread(A(n("W") + "s", P + a0, P + a0 + KO), "new%ds" % t)
 
     def newlist(t):
         n = lambda s: s + str(t)
-        w, mo = n("w"), n("mo")
-        tt(A(w, 0, 64), A(n("lk"), 0, 64), A("mk", 0, 64), OP.mult)
-        tt(A(w, 136, 140), A(n("jf"), 0, 4), A("dkw", 0, 4), OP.subtract)
-        scan(A(w, 64, 128), A("sd", 0, 64), A(w, 0, 64), OP.mult, OP.add)
-        ts(A(w, 132, 136), A(w, 79, 128, 16), float(rank - 8), None, OP.is_equal)
-        tt(A(w, 140, 144), A(w, 132, 136), A(w, 136, 140), OP.mult)
-        tt(A(w, 144, 148), A(w, 140, 144), A("dkw", 0, 4), OP.add)
-        cp("v", A(mo, 0, 4), A(w, 144, 148))
-        scatter(A(n("M"), 0, 384), A(mo, 0, 4), A("nat", P, P + K))
-        m, mmx = n("M"), n("mm")
-        cut = rank if t == 0 else P - rank if rank else 0
-        tt(A(mmx, 0, P - cut), A(m, cut, P), A("mk", 0, P - cut), OP.mult)
-        if cut:
-            tt(A(mmx, P - cut, P), A(m, 0, cut), A("mk", P - cut, P), OP.mult)
-        scan(A(mmx, 256, 512), A("sd", 0, 256), A(mmx, 0, 256), OP.mult, OP.add)
-        cp("v", A(n("ml"), 0, 16), A(mmx, 256 + 15, 512, 16))
+        gather("s", A(n("wg"), 0, 64), A(n("xm"), 0, 256), A(n("of"), 0, 4))
+        gather("s", A(n("wa"), 0, 64), A(n("M"), 0, 256), A(n("of"), 0, 4))
+        tt(A(n("wb"), 0, 64), A(n("wg"), 0, 64), A("nat", P, P + K), OP.mult)
+        ts(A(n("wd"), 0, 64), A(n("lk"), 0, 64), float(rank - 8), None, OP.is_equal)
+        tt(A(n("wc"), 0, 64), A(n("wb"), 0, 64), A(n("wa"), 0, 64), OP.subtract)
+        tt(A(n("we"), 0, 64), A(n("wd"), 0, 64), A(n("wc"), 0, 64), OP.mult)
+        tt(A(n("wf"), 0, 64), A(n("we"), 0, 64), A(n("wa"), 0, 64), OP.add)
+        scatter(A(n("M"), 0, 256), A(n("of"), 0, 4), A(n("wf"), 0, 64))
+        m, mmx, c = n("M"), n("mm"), shift(t)
+        scan(A(mmx, 0, P - c), A("sd", 0, P - c), A(m, c, P), OP.mult, OP.add)
+        if c:
+            scan(A(mmx, P - c, P), A("sd", P - c, P), A(m, 0, c), OP.mult, OP.add, A(mmx, P - c - 1, P - c))
+        cp("v", A(n("ml"), 0, 16), A(mmx, 15, 256, 16))
 
     def finish(t):
         n = lambda s: s + str(t)
         if own == t:
             rebuild(t)
         if t == 0:
-            act(A("xa", 0, 256), A("x16", 0, 256), AF.Abs, bias=A("ng", 1, 2))
-            act(A("mk", 0, 256), A("xa", 0, 256), AF.Relu, bias=1.0, scale=-1.0)
-            act(A("sd", 0, 256), A("x16", 0, 256), AF.Sign)
-            ts(A("dkw", 0, 4), A("dk", 0, 4), A("fb", 3, 4), None, OP.add)
-        cp("s", A(n("M"), 0, P), A("nat", 0, P))
-        lists(t)
+            tt(A("M0", 0, P), A("xm0", 0, P), A("nat", 0, P), OP.mult)
         newlist(t)
+        lists(t)
         if t == 0:
-            quant("W0", 0, 256, "tbt", 0)
-            ts(A("ma1", 0, 16), A("rc", 0, 16), A("fb", 1, 2), -1.0, OP.is_equal, OP.mult)
-            ts(A("mb1", 0, 16), A("rc", 0, 16), A("fb", 1, 2), None, OP.not_equal)
-            act(A("D1", 0, 256), A("nat", 0, 256), AF.Copy, scale=0.0)
+            const(A("D1", 0, 256), 0.0, A("nat", 0, 256))
             if own:
                 owner()
-                for b in range(4):
-                    unit(b)
+                owner_v()
         others = [o for o in range(NO) if 2 * o + t != rank]
-        landed([A(n("W") + s, P + KO * o, P + KO * o + KO) for o in others for s in ("", "s")], "new%d" % t, len(others) * 2 * full)
+        for s in ("", "s"):
+            landed([A(n("W") + s, P + KO * o, P + KO * o + KO) for o in others], "new%d" % t + s, len(others) * full)
 
-    judge(0, "tA")
+    def after():
+        if own == 0:
+            owner()
+        act(A("ng", 1, 2), A("fb", 3, 4), AF.Copy, scale=-1.0)
+        lanes(0)
+        act(A("sd", 0, 256), A("x16", 0, 256), AF.Sign)
+
+    judge(0, "tA", after)
     finish(0)
-    checks(1, "tB", lambda h: pick("tB", 128 * h, 128 * h + 128, "W0", P + K, A("ml0", 8 * h, 8 * h + 8)))
+    pick2("tB", 128, "W0", P + K, "ml0", 8)
+    checks(1, "tB", lambda h: None, "s")
     pick("W1", 0, P, "W0", P + K, A("ml0", 0, 16))
+    masks(1)
     quant("wq", 0, 128, "wt", 0)
-    judge(1, "tB")
+    lanes(1)
+    tt(A("M1", 0, P), A("xm1", 0, P), A("nat", 0, P), OP.mult)
+    judge(1, "tB", lambda: None)
     finish(1)
+    pick2("F", 128, "W1", P + K, "ml1", 8)
     for h in range(2):
-        pick("F", 128 * h, 128 * h + 128, "W1", P + K, A("ml1", 8 * h, 8 * h + 8))
         mm(A("py", 512 * h, 512 * h + 128), "wq", 0, "F", 128 * h, 128 * h + 128)
         dma("y", None, A("F", 128 * h, 128 * h + 128), "st_c", 32, out_ap=T.oc[:, 512 * h:512 * h + 512],
             in_ap=T.F[:, 128 * h:128 * h + 128].bitcast(dt.uint8))
+    for k in range(4):
+        dma("y", None, A("Fs", 0, P, 1, 32 * k, 32 * k + 4), "st_s", 64, out_ap=T.osc[4 * k:4 * k + 4, :])
     cp("v", A("yb", 0, 128), A("py", 0, 128))
     cp("s", A("yb", 128, 256), A("py", 512, 640))
     dma("y", None, A("yb", 0, 128), "st_y", 32, out_ap=T.y[:, 0:128])
     dma("s", None, A("yb", 128, 256), "st_y", 32, out_ap=T.y[:, 128:256])
-    for k in range(4):
-        dma("s" if k % 2 else "y", None, A("Fs", 0, P, 1, 32 * k, 32 * k + 4), "st_s", 64, out_ap=T.osc[4 * k:4 * k + 4, :])
     for sem, val in final.items():
         wait("g", sem, val)

@@ -8,7 +8,7 @@ N, P, K, NO, KO = 8, 256, 64, 4, 16
 BIG = 1e29
 STEP = 1.0 - 2.0 ** -24
 TINY = 2.0 ** -118
-FR = 2.0 ** -10
+FR = 2.0 ** -8
 
 F4 = "float8_e4m3fn_x4"
 SCRATCH = {}
@@ -34,28 +34,30 @@ def _parts(buf, *parts):
 
 for _n, _w in (("tbt", 4 * P), ("ut", 512), ("wt", 512), ("ee", 528), ("zt", 512)):
     _sb(_n, _w, "bfloat16")
-_parts("con", ("rc", 32), ("hm", 32), ("jc", 1), ("ad", 4), ("ad2", 4), ("hb", 128), ("hx", 32), ("hp", 32), ("hq", 32), ("hr", 32),
-       ("kl0", 8), ("dl0", 8), ("fb", 5), ("fc", 3), ("u1", 2), ("sd32", 32), ("sp", 16), ("one", 32), ("oc", 8), ("klc", 8),
-       ("ng", 4), ("ae", 4), ("eq0", 32), ("eq1", 32), ("dm0", 32), ("dm1", 32), ("gm0", 16), ("gm1", 16), ("lof", 4))
-for _n, _w in (("nat", 528), ("ea", 528), ("x16", 272), ("xa0", 256), ("xa1", 256), ("xm0", 256), ("xm1", 256), ("q8", 264), ("qn", 256),
-               ("jp", 128), ("md", 132), ("vj", 128), ("sd", 256), ("dpat", 128), ("yb", 256)):
+_parts("con", ("rc", 40), ("hm", 32), ("jc", 1), ("hx", 32), ("hy", 32), ("rf", 40), ("dl0", 8), ("fb", 8), ("st", 2), ("sd32", 32),
+       ("sp", 16), ("one", 32), ("frc", 32), ("oc", 8), ("klc", 16), ("ng", 4), ("eq0", 32), ("eq1", 32), ("dm0", 32), ("dm1", 32),
+       ("gm0", 16), ("gm1", 16), ("lof", 4), ("vj0", 32), ("vj1", 32), ("pr", 64), ("l16", 64), ("t3", 64), ("t4", 64), ("t5", 64),
+       ("t6", 64), ("t7", 64), ("t8", 64))
+for _n, _w in (("nat", 528), ("x16", 272), ("xa0", 256), ("xa1", 256), ("xm0", 256), ("xm1", 256), ("md", 128),
+               ("sd", 256), ("dpat", 128), ("yb", 256), ("ya", P + K), ("lt", 64), ("wt01", 64), ("tab", 128)):
     _sb(_n, _w)
 _sb("pi", 2, "int32")
-_sb("ib", 5, "int32")
-_sb("id", 3, "int32")
+_sb("ib", 8, "int32")
 _sb("cl", 2, "uint16")
 _sb("lo", 4, "uint16")
 _sb("dl", 8, "uint16")
+_sb("gl", 2, "uint16")
 for _n, _w in (("tA", P), ("tB", P), ("F", P), ("uq", 128), ("wq", 128), ("eq", 512)):
     _mx(_n, _w)
 for _t in "01":
     _parts("jd" + _t, ("d1" + _t, 32), ("so" + _t, 32), ("du" + _t, 64), ("lw" + _t, 32), ("px" + _t, 16), ("tl" + _t, 64), ("rk" + _t, 4),
-           ("tt" + _t, 128), ("xb" + _t, 4), ("jf" + _t, 4), ("fr" + _t, 4), ("ol" + _t, 128), ("wg" + _t, 64), ("wa" + _t, 64),
-           ("wb" + _t, 64), ("wc" + _t, 64), ("wd" + _t, 64), ("we" + _t, 64), ("wf" + _t, 64), ("th" + _t, 264), ("cm" + _t, 260),
-           ("ca" + _t, 2), ("cb" + _t, 2), ("ls" + _t, 2), ("rl" + _t, 256), ("cj" + _t, 256), ("lj" + _t, 16), ("mm" + _t, 256))
-    for _n, _w in (("L", 32), ("S", 256), ("Lz", 256), ("D", 256), ("dd", 128), ("bk", 64), ("lk", 64), ("lr", 64), ("qk", 64), ("M", 256)):
+           ("tt" + _t, 128), ("xs" + _t, 8), ("ys" + _t, 8), ("xb" + _t, 4), ("jf" + _t, 4), ("fr" + _t, 4), ("zz" + _t, 16),
+           ("zo" + _t, 8), ("nd" + _t, 1), ("wg" + _t, 64), ("wb" + _t, 64), ("wc" + _t, 64), ("wd" + _t, 64), ("we" + _t, 64),
+           ("wf" + _t, 64), ("th" + _t, 256), ("cm" + _t, 260), ("ca" + _t, 2), ("cb" + _t, 2), ("ls" + _t, 2), ("rl" + _t, 256),
+           ("cj" + _t, 256), ("lj" + _t, 16), ("mm" + _t, 256))
+    for _n, _w in (("L", 32), ("S", 256), ("Lz", 64), ("val", 32), ("D", 256), ("dd", 128), ("bk", 64), ("lk", 64), ("M", 256)):
         _sb(_n + _t, _w)
-    for _n, _w in (("R", 8), ("of", 4), ("op", 4), ("oo", 2), ("ml", 16), ("oi", 8)):
+    for _n, _w in (("R", 2), ("of", 4), ("cd", 4), ("oo", 2), ("lc", 2), ("ml", 16), ("oi", 8)):
         _sb(_n + _t, _w, "uint16")
     _sb("h" + _t, 512, "bfloat16")
     for _n, _w in (("slot", K), ("land", 256), ("ord", 128), ("new", 128), ("W", P + K)):
@@ -184,6 +186,9 @@ def rank_program(g, core, T, topo):
         else:
             op("s", [out], [win, off], lambda: g.scalar.activation(out[4], win[4].indirect(off[4]), f))
 
+    def gather_tt(out, win, off, b, o):
+        op("v", [out], [win, off, b], lambda: g.vector.tensor_tensor(out[4], win[4].indirect(off[4]), b[4], o))
+
     def scatter(win, off, val):
         op("v", [win], [val, off], lambda: g.vector.tensor_copy(win[4].indirect(off[4]), val[4]))
 
@@ -266,14 +271,19 @@ def rank_program(g, core, T, topo):
 
     iota(A("pi", 0, 2), [[1, 2]], 0, 1, False)
     iota(A("nat", 0, 128), [[1, 128]], 0, 0)
-    iota(A("rc", 0, 32), [[0, 4], [1, 8]], 0, 0)
+    iota(A("rc", 0, 40), [[0, 5], [1, 8]], 0, 0)
     iota(A("hm", 0, 32), [[0, 2], [1, 2], [0, 8]], 0, 0)
     iota(A("jc", 0, 1), [[1, 1]], 0, 1)
+    iota(A("lt", 0, 64), [[0, 8], [1, 8]], 0, 0)
+    iota(A("pr", 0, 64), [[16, 8], [0, 8]], 0, 0)
+    iota(A("hx", 0, 32), [[128, 2], [1, 16]], 0, 0)
+    iota(A("dl0", 0, 8), [[16, 4], [0, 2]], 0, 0)
     fill(A("ut", 8, 512), 0.0)
     fill(A("one", 0, 32), 1.0)
-    for col, (src, bits) in enumerate(((0, 7), (1, 7), (0, 16), (0, 15), (0, 8))):
+    fill(A("frc", 0, 32), FR)
+    for col, (src, bits) in enumerate(((0, 7), (1, 7), (0, 31), (0, 15), (0, 8), (0, 112), (0, 64), (0, 32))):
         ts(A("ib", col, col + 1), A("pi", src, src + 1), bits, None, OP.bitwise_and)
-    cp("v", A("fb", 0, 5), A("ib", 0, 5))
+    cp("v", A("fb", 0, 8), A("ib", 0, 8))
 
     def masks(t):
         n = str(t)
@@ -286,9 +296,7 @@ def rank_program(g, core, T, topo):
     act(A("nat", 128, 256), A("nat", 0, 128), AF.Identity, bias=128.0)
     act(A("nat", 256, 512), A("nat", 0, 256), AF.Identity, bias=256.0)
     act(A("nat", 512, 528), A("nat", 0, 16), AF.Identity, bias=512.0)
-    act(A("ng", 0, 1), A("jc", 0, 1), AF.Identity, bias=-4.0, scale=-4.0)
-    act(A("ea", 0, 528), A("nat", 0, 528), AF.Abs, bias=A("ng", 0, 1))
-    act(A("ee", 0, 528), A("ea", 0, 528), AF.Relu, bias=1.0, scale=-1.0)
+    act(A("ng", 0, 1), A("jc", 0, 1), AF.Identity, bias=4.0, scale=4.0)
 
     def checks(t, tab, half, e0):
         for h in range(2):
@@ -301,70 +309,74 @@ def rank_program(g, core, T, topo):
 
     checks(0, "tA", lambda h: quant("tA", 128 * h, 128 * h + 128, "tbt", 512 * h), "v")
 
-    iota(A("hb", 0, 128), [[0, 4], [1, 32]], 0, 0)
-    iota(A("hx", 0, 32), [[128, 2], [1, 16]], 0, 0)
-    iota(A("hp", 0, 32), [[32, 2], [1, 16]], 0, 0)
-    iota(A("dl0", 0, 8), [[16, 4], [0, 2]], 0, 0)
+    iota(A("D0", 0, 256), [[0, 256]], 0, 0)
     iota(A("x16", 0, 272), [[0, 17], [1, 16]], 0, 0)
-    iota(A("q8", 0, 264), [[0, 33], [1, 8]], 0, 0)
-    iota(A("kl0", 0, 8), [[2, 8]], 0, 0)
-    for col, bits in enumerate((96, 64, 32)):
-        ts(A("id", col, col + 1), A("pi", 0, 1), bits, None, OP.bitwise_and)
-    cp("v", A("fc", 0, 3), A("id", 0, 3))
+    iota(A("D1", 0, 256), [[0, 256]], 0, 0)
     ts(A("lo", 0, 1), A("fb", 0, 1), 4.0, None, OP.mult)
     ts(A("lo", 1, 2), A("fb", 0, 1), 4.0, 2.0, OP.mult, OP.add)
-    cp("s", A("ad", 0, 1), A("fc", 0, 1))
-    act(A("u1", 0, 1), A("fc", 1, 2), AF.Identity, bias=64.0, scale=-1.0)
-    act(A("u1", 1, 2), A("fc", 2, 3), AF.Identity, bias=32.0, scale=-1.0)
-    act(A("ad", 3, 4), A("fc", 0, 1), AF.Identity, bias=96.0, scale=-1.0)
-    act(A("ad", 1, 2), A("u1", 0, 1), AF.Identity, bias=A("fc", 2, 3))
-    act(A("ad", 2, 3), A("u1", 1, 2), AF.Identity, bias=A("fc", 1, 2))
-    for s in range(4):
-        act(A("jp", 32 * s, 32 * s + 32), A("hb", 32 * s, 32 * s + 32), AF.Identity, bias=A("ad", s, s + 1))
     act(A("lof", 0, 1), A("fb", 4, 5), AF.Identity, bias=1.0, scale=0.25)
     act(A("lof", 1, 2), A("fb", 0, 1), AF.Identity, bias=A("lof", 0, 1), scale=4.0)
-    act(A("ad2", 0, 1), A("fb", 2, 3), AF.Copy, scale=1.0 + FR)
-    act(A("hq", 0, 32), A("hp", 0, 32), AF.Copy, scale=FR)
-    act(A("ae", 0, 4), A("ad", 0, 4), AF.Identity, bias=A("ad2", 0, 1))
-    const(A("md", 128, 129), -1.0, A("nat", 0, 1))
     cp("s", A("sd32", 0, 32), A("one", 0, 32))
     const(A("sd32", 0, 32, 16), 0.0, A("nat", 0, 2))
-    for t in "01":
-        const(A("cm" + t, 256, 257), 128.0, A("nat", 0, 1))
     const(A("sp", 0, 16), 0.0, A("nat", 0, 16))
     const(A("sp", 0, 16, 8), -BIG, A("nat", 0, 2))
-    const(A("D0", 0, 256), 0.0, A("nat", 0, 256))
+    act(A("rf", 0, 40), A("rc", 0, 40), AF.Copy, scale=8.0 * FR)
+    for t in "01":
+        const(A("cm" + t, 256, 257), 128.0, A("nat", 0, 1))
 
     def owner():
-        cp("s", A("qn", 0, 256), A("q8", own, own + 256))
-        act(A("oc", 3, 4), A("fb", 4, 5), AF.Copy, scale=0.125)
-        act(A("oc", 0, 1), A("fb", 0, 1), AF.Identity, bias=-1.0)
-        act(A("oc", 1, 2), A("fb", 0, 1), AF.Relu, bias=-1.0)
+        act(A("oc", 0, 1), A("fb", 0, 1), AF.Identity, bias=-16.0, scale=16.0)
+        act(A("oc", 1, 2), A("fb", 0, 1), AF.Relu, bias=-16.0, scale=16.0)
         act(A("oc", 2, 3), A("fb", 0, 1), AF.Relu, bias=1.0, scale=-1.0)
-        act(A("oc", 4, 5), A("fb", 4, 5), AF.Identity, bias=-8.0, scale=12.5)
-        act(A("oc", 5, 6), A("fb", 4, 5), AF.Identity, bias=92.0, scale=-12.5)
-        act(A("oc", 6, 7), A("fb", 4, 5), AF.Copy, scale=0.125 / 128)
-        act(A("klc", 0, 8), A("kl0", 0, 8), AF.Identity, bias=A("oc", 6, 7), scale=1.0 / 128)
+        act(A("oc", 3, 4), A("fb", 4, 5), AF.Copy, scale=0.125)
+        act(A("oc", 4, 5), A("fb", 4, 5), AF.Identity, bias=1.0, scale=-0.125)
+        act(A("oc", 5, 6), A("fb", 4, 5), AF.Copy, scale=8.0)
+        act(A("oc", 6, 7), A("fb", 4, 5), AF.Identity, bias=7.0)
+        act(A("klc", 0, 8), A("nat", 0, 8), AF.Copy, scale=A("oc", 4, 5))
+        act(A("klc", 8, 16), A("nat", 8, 16), AF.Copy, scale=A("oc", 3, 4))
+        act(A("l16", 0, 64), A("lt", 0, 64), AF.Copy, scale=16.0)
+        act(A("t4", 0, 64), A("pr", 0, 64), AF.Identity, bias=A("oc", 1, 2), scale=A("oc", 2, 3))
+        const(A("dpat", 0, 128), 1.0, A("nat", 0, 128))
+        const(A("dpat", 0, 128, 8), 0.0, A("nat", 0, 16))
+        const(A("dpat", 1, 128, 8), -1.0, A("nat", 0, 16))
 
     def owner_v():
         fill(A("zt", 0, 512), 0.0)
-        fill(A("dpat", 0, 128), 1.0)
-        ts(A("cl", 0, 1), A("fb", 3, 4), 8.0, 7.0, OP.mult, OP.add)
-        fill(A("dpat", 0, 128, 8), 0.0)
-        fill(A("dpat", 1, 128, 8), -1.0)
+        ts(A("ee", 0, 528), A("nat", 0, 528), A("ng", 0, 1), None, OP.is_equal)
         quant("land%d" % own, 128, 256, "zt", 0)
         for b in range(4):
             quant("eq", 128 * b, 128 * b + 128, "ee", 4 - b)
+        ts(A("cl", 0, 1), A("fb", 0, 1), 16.0, A("oc", 6, 7), OP.mult, OP.add)
 
-    quant("W0", 0, 256, "tbt", 0)
-    if own == 0:
-        owner_v()
+    def owner_t():
+        ts(A("t3", 0, 64), A("pr", 0, 64), A("oc", 0, 1), 16.0, OP.is_le, OP.mult)
+        tt(A("t5", 0, 64), A("t3", 0, 64), A("t4", 0, 64), OP.add)
+        tt(A("t6", 0, 64), A("t5", 0, 64), A("l16", 0, 64), OP.is_equal)
+        act(A("t7", 0, 64), A("t6", 0, 64), AF.Copy, scale=128.0)
+        tt(A("t8", 0, 64), A("t5", 0, 64), A("t7", 0, 64), OP.add)
+        act(A("tab", 0, 64), A("t8", 0, 64), AF.Copy, scale=A("oc", 4, 5))
+        act(A("tab", 64, 128), A("t8", 0, 64), AF.Copy, scale=A("oc", 3, 4))
+
     cp("v", A("lo", 2, 3), A("lof", 1, 2))
-    ts(A("md", 0, 128), A("jp", 0, 128), A("jc", 0, 1), STEP, OP.is_ge, OP.max)
-    tt(A("hr", 0, 32), A("hq", 0, 32), A("hx", 0, 32), OP.add)
-    for s in range(4):
-        ts(A("vj", 32 * s, 32 * s + 32), A("hr", 0, 32), A("ae", s, s + 1), 64.0 * FR * s, OP.add, OP.add)
+    ts(A("gl", 0, 1), A("fb", 2, 3), 0.0, None, OP.add)
+    ts(A("gl", 1, 2), A("fb", 2, 3), 32.0, None, OP.add)
+    if own == 0:
+        owner()
+        owner_v()
+    else:
+        quant("W0", 0, 256, "tbt", 0)
+    act(A("st", 0, 1), A("fb", 6, 7), AF.Identity, bias=1.0, scale=(STEP - 1.0) / 64)
+    act(A("st", 1, 2), A("fb", 7, 8), AF.Identity, bias=1.0, scale=(STEP - 1.0) / 32)
+    for s, c in ((1, 0), (2, 1), (3, 0)):
+        act(A("md", 32 * s, 32 * s + 32), A("one", 0, 32), AF.Copy, scale=A("st", c, c + 1))
+    ts(A("md", 0, 32), A("nat", 0, 32), A("fb", 2, 3), STEP, OP.is_ge, OP.max)
     ts(A("dl", 0, 8), A("dl0", 0, 8), A("fb", 3, 4), None, OP.add)
+    ts(A("hy", 0, 32), A("hx", 0, 32), A("fb", 5, 6), None, OP.add)
+    for t in range(2):
+        tt(A("vj%d" % t, 0, 32), A("hy", 0, 32), A("rf", t, t + 32), OP.add)
+    if own == 0:
+        owner_t()
+    ts(A("wt01", 0, 64), A("lt", 0, 64), float(rank), None, OP.is_equal)
 
     def shift(t):
         return rank if t == 0 else -rank % P
@@ -374,109 +386,82 @@ def rank_program(g, core, T, topo):
         act(A("xa" + n, 0, 256), A("x16", c, c + 256), AF.Abs, bias=A("ng", 1, 2))
         act(A("xm" + n, 0, 256), A("xa" + n, 0, 256), AF.Relu, bias=1.0, scale=-1.0)
 
-    def across(buf, v):
-        cp("v", A(buf, 64, 128, 1, 0, 64), A(buf, 0, 64, 1, 64, 128))
-        cp("s", A(buf, 64, 128, 1, 64, 128), A(buf, 0, 64, 1, 0, 64))
-
-        def rest(e, a1, a2):
-            for a in range(a1, a2):
-                b = a ^ 1
-                cp(e, A(buf, 128, 256, 1, 32 * a, 32 * a + 32), A(buf, 0, 128, 1, 32 * b, 32 * b + 32))
-        rest("s", v, 4)
-        return lambda: rest("v", 0, v)
-
-    def judge(t, tab, meanwhile):
+    def judge(t, tab):
         n = lambda s: s + str(t)
         L, d1, so, du, S, lw, px, tl = n("L"), n("d1"), n("so"), n("du"), n("S"), n("lw"), n("px"), n("tl")
         th, cm, cj, rl, ca, cb, ls, rk, R = n("th"), n("cm"), n("cj"), n("rl"), n("ca"), n("cb"), n("ls"), n("rk"), n("R")
-        o, i, f, m = A(d1, 0, 32), A(L, 0, 32), A("lo", 0, 2), A(n("dm"), 0, 32)
-        op("v", [o], [i, f, m], lambda: g.vector.tensor_tensor(o[4], i[4].indirect(f[4]), m[4], OP.mult))
+        i = A(L, 0, 32)
+        gather_tt(A(d1, 0, 32), i, A("lo", 0, 2), A(n("dm"), 0, 32), OP.mult)
         gather("s", A(lw, 0, 16), i, A("lo", 2, 3), AF.Abs)
         scan(A(so, 0, 32), A("sd32", 0, 32), A(d1, 0, 32), OP.mult, OP.subtract)
         for h in range(2):
             act(A(du, 32 * h, 32 * h + 32), A("one", 0, 32), AF.Abs, bias=TINY, scale=A(so, 16 * h + 15, 16 * h + 16))
-        for h in range(2):
-            act(A(th, 132 * h, 132 * h + 129), A("md", 0, 129), AF.Copy, scale=A(du, 32 * h, 32 * h + 1))
         tt(A(lw, 16, 32), A(lw, 0, 16), A(n("gm"), 0, 16), OP.subtract)
         scan(A(px, 0, 16), A("sp", 0, 16), A(lw, 16, 32), OP.add, OP.max)
         for h in range(2):
             turn(A(S, 128 * h, 128 * h + 32), A(du, 32 * h, 32 * h + 32))
-        for h in (0, 128):
-            cp("v", A(S, h + 32, h + 64, 1, 0, 64), A(S, h, h + 32, 1, 64, 128))
-            cp("s", A(S, h + 32, h + 64, 1, 64, 128), A(S, h, h + 32, 1, 0, 64))
-        for h in (0, 128):
-            for a, e in ((0, "v"), (2, "s"), (1, "v"), (3, "s")):
-                b = a ^ 1
-                cp(e, A(S, h + 64, h + 128, 1, 32 * a, 32 * a + 32), A(S, h, h + 64, 1, 32 * b, 32 * b + 32))
-        act(A(rl, 0, 128), A(S, 128, 256), AF.Relu, bias=A(th, 128, 129))
-        act(A(rl, 128, 256), A(S, 0, 128), AF.Relu, bias=A(du, 32, 33), scale=-1.0)
-        act(A(cj, 0, 128), A(rl, 0, 128), AF.Sign, total=A(ca, 0, 1))
-        act(A(cj, 128, 256), A(rl, 128, 256), AF.Sign, scale=-1.0, total=A(ca, 1, 2))
         for h in range(2):
             act(A(n("lj"), 8 * h, 8 * h + 8), A(px, 8 * h, 8 * h + 8), AF.Sign, bias=A(px, 8 * h + 7, 8 * h + 8), scale=-1.0,
                 total=A(ls, h, h + 1))
         for h in range(2):
-            act(A(tl, 32 * h, 32 * h + 32), A("one", 0, 32), AF.Identity, bias=-8.0, scale=A(ls, h, h + 1))
-        meanwhile()
-        for h in range(2):
-            tt(A(cm, 128 * h, 128 * h + 128), A(S, 128 * h, 128 * h + 128), A(th, 132 * h, 132 * h + 128), OP.is_gt)
-        red(A(cb, 0, 1), A(cm, 0, 128), OP.add)
+            act(A(tl, 32 * h, 32 * h + 32), A("frc", 0, 32), AF.Copy, scale=A(ls, h, h + 1))
+        for h in (0, 128):
+            cp("v", A(S, h + 32, h + 64, 1, 0, 64), A(S, h, h + 32, 1, 64, 128))
+            cp("s", A(S, h + 32, h + 64, 1, 64, 128), A(S, h, h + 32, 1, 0, 64))
+        ts(A(th, 128, 256), A("md", 0, 128), A(du, 32, 33), None, OP.mult)
+        for h in (0, 128):
+            for a, e in ((0, "v"), (2, "s"), (1, "v"), (3, "s")):
+                b = a ^ 1
+                cp(e, A(S, h + 64, h + 128, 1, 32 * a, 32 * a + 32), A(S, h, h + 64, 1, 32 * b, 32 * b + 32))
+        turn(A(n("Lz"), 0, 64), A(tl, 0, 64))
+        gather_tt(A(n("val"), 0, 32), A(n("Lz"), 0, 64), A("gl", 0, 2), A("vj%d" % t, 0, 32), OP.add)
+        act(A(th, 0, 128), A("md", 0, 128), AF.Copy, scale=A(du, 0, 1))
+        act(A(n("nd"), 0, 1), A(du, 0, 1), AF.Copy, scale=-1.0)
+        act(A(rl, 128, 256), A(S, 0, 128), AF.Relu, bias=A(du, 32, 33), scale=-1.0)
+        act(A(rl, 0, 128), A(S, 128, 256), AF.Relu, bias=A(n("nd"), 0, 1))
+        act(A(cj, 128, 256), A(rl, 128, 256), AF.Sign, scale=-1.0, total=A(ca, 1, 2))
+        act(A(cj, 0, 128), A(rl, 0, 128), AF.Sign, total=A(ca, 0, 1))
+        for h in (1, 0):
+            tt(A(cm, 128 * h, 128 * h + 128), A(S, 128 * h, 128 * h + 128), A(th, 128 * h, 128 * h + 128), OP.is_gt)
         red(A(cb, 1, 2), A(cm, 128, 257), OP.add)
+        red(A(cb, 0, 1), A(cm, 0, 128), OP.add)
         tt(A(rk, 0, 2), A(ca, 0, 2), A(cb, 0, 2), OP.add)
-        tt(A(rk, 2, 4, 1, 0, 64), A(ca, 0, 2, 1, 64, 128), A(cb, 0, 2, 1, 64, 128), OP.add)
-        tt(A(rk, 2, 4, 1, 64, 128), A(ca, 0, 2, 1, 0, 64), A(cb, 0, 2, 1, 0, 64), OP.add)
-        cp("v", A(R, 0, 4), A(rk, 0, 4))
-        for a in range(4):
-            b = a ^ 1
-            cp("v", A(R, 4, 8, 1, 32 * a, 32 * a + 32), A(rk, 0, 4, 1, 32 * b, 32 * b + 32))
-        scatter(A(n("D"), 0, 256), A(R, 0, 8), A("vj", 0, 128))
+        cp("v", A(R, 0, 2), A(rk, 0, 2))
+        scatter(A(n("D"), 0, 256), A(R, 0, 2), A(n("val"), 0, 32))
         gather("v", A(n("dd"), 0, 128), A(n("D"), 0, 64), A("dl", 0, 8))
         turn(A(n("tt"), 0, 128), A(n("dd"), 0, 128))
-        xb, of = n("xb"), n("of")
-        tt(A(xb, 0, 4), A(n("tt"), 0, 128, 32), A(n("tt"), 16, 128, 32), OP.add)
+        xs, ys, xb, of = n("xs"), n("ys"), n("xb"), n("of")
+        tt(A(xs, 0, 4), A(n("tt"), 0, 128, 32), A(n("tt"), 16, 128, 32), OP.add)
+        cp("v", A(xs, 4, 8, 1, 0, 64), A(xs, 0, 4, 1, 64, 128))
+        cp("s", A(xs, 4, 8, 1, 64, 128), A(xs, 0, 4, 1, 0, 64))
+        tt(A(ys, 0, 4), A(xs, 0, 4), A(xs, 4, 8), OP.add)
+        for a, e in ((0, "v"), (2, "s"), (1, "v"), (3, "s")):
+            b = a ^ 1
+            cp(e, A(ys, 4, 8, 1, 32 * a, 32 * a + 32), A(ys, 0, 4, 1, 32 * b, 32 * b + 32))
+        tt(A(xb, 0, 4), A(ys, 0, 4), A(ys, 4, 8), OP.add)
         cp("v", A(of, 0, 4), A(xb, 0, 4))
         pick(n("slot"), 0, K, tab, P, A(of, 0, 4))
         deal(t, True)
         deal(t, False)
-        turn(A(n("Lz"), 0, 64), A(tl, 0, 64))
-        more = across(n("Lz"), 2 if own != t else 0)
-        v = lambda i: A(n("ol"), 8 * i, 8 * i + 8)
-        if own == t:
-            even, odd = A(n("qk"), a0, a0 + 16, 2), A(n("qk"), a0 + 1, a0 + 16, 2)
-            gather("v", A(n("qk"), 0, 64), A("qn", 0, 256), A(of, 0, 4))
-            cp("v", A(n("oo"), 0, 1), A(xb, o_, o_ + 1))
-            tt(v(0), odd, even, OP.subtract)
-            pick(n("land"), KO * rank, KO * rank + KO, tab, P, A(n("oo"), 0, 1))
-            ts(v(1), v(0), A("oc", 3, 4), None, OP.mult)
         cp("v", A(n("jf"), 0, 4), A(of, 0, 4))
         if own == t:
-            tt(v(2), v(1), even, OP.add)
+            cp("v", A(n("oo"), 0, 1), A(xb, o_, o_ + 1))
+            pick(n("land"), KO * rank, KO * rank + KO, tab, P, A(n("oo"), 0, 1))
         tt(A(n("fr"), 0, 4), A(xb, 0, 4), A(n("jf"), 0, 4), OP.subtract)
         if own == t:
-            ts(v(3), v(2), A("oc", 0, 1), None, OP.is_le)
-            ts(v(4), v(2), A("oc", 2, 3), A("oc", 1, 2), OP.mult, OP.add)
-        ts(A(n("op"), 0, 4), A(n("fr"), 0, 4), 1.0 / FR, None, OP.mult)
-        more()
-        if own == t:
-            tt(v(5), v(3), v(4), OP.add)
-        gather("v", A(n("lk"), 0, 64), A(n("Lz"), 0, 256), A(n("op"), 0, 4))
-        if own == t:
-            act(v(6), v(5), AF.Identity, bias=A("oc", 4, 5))
-            act(v(7), v(5), AF.Identity, bias=A("oc", 5, 6))
-            act(v(8), v(5), AF.Copy, scale=KO / 128.0)
-            tt(v(10), v(6), A(n("lk"), a0, a0 + 16, 2), OP.is_equal)
-            tt(v(11), v(7), A(n("lk"), a0 + 1, a0 + 16, 2), OP.is_equal)
-            tt(v(9), v(8), A("klc", 0, 8), OP.add)
-            tt(v(12), v(10), v(11), OP.add)
-            tt(v(13), v(12), v(9), OP.add)
-            ts(A(n("oi"), 0, 8), v(13), 128.0, None, OP.mult)
+            ts(A(n("lc"), 0, 1), A(n("fr"), o_, o_ + 1), 1.0 / FR, A("oc", 5, 6), OP.mult, OP.add)
+            gather_tt(A(n("zz"), 0, 16), A("tab", 0, 128), A(n("lc"), 0, 1), A("klc", 0, 16), OP.add)
+            tt(A(n("zo"), 0, 8), A(n("zz"), 0, 8), A(n("zz"), 8, 16), OP.add)
+            cp("v", A(n("oi"), 0, 8), A(n("zo"), 0, 8))
+        ts(A(n("cd"), 0, 4), A(n("fr"), 0, 4), 1.0 / FR, None, OP.mult)
+        gather("s", A(n("bk"), 0, 64), A("nat", 0, 256), A(of, 0, 4))
+        gather("s", A(n("wd"), 0, 64), A("wt01", 0, 64), A(n("cd"), 0, 4))
 
     def lists(t):
         n = lambda s: s + str(t)
-        gather("s", A(n("bk"), 0, 64), A("nat", 0, 256), A(n("of"), 0, 4))
-        act(A(n("lr"), 0, 64), A(n("lk"), 0, 64), AF.Identity, bias=8.0)
+        gather("s", A(n("lk"), 0, 64), A("lt", 0, 64), A(n("cd"), 0, 4))
         dma("y", None, A(n("bk"), 0, 64, 1, 0, 1), "st_b%d" % t, 32, out_ap=T.bs[2 * t:2 * t + 1, :])
-        dma("y", None, A(n("lr"), 0, 64, 1, 0, 1), "st_b%d" % t, 32, out_ap=T.bs[2 * t + 1:2 * t + 2, :])
+        dma("y", None, A(n("lk"), 0, 64, 1, 0, 1), "st_b%d" % t, 32, out_ap=T.bs[2 * t + 1:2 * t + 2, :])
 
     def rebuild(t):
         n = lambda s: s + str(t)
@@ -492,15 +477,16 @@ def rank_program(g, core, T, topo):
         spread(A(n("W"), P + a0, P + a0 + KO), "new%d" % t, True)
         spread(A(n("W") + "s", P + a0, P + a0 + KO), "new%ds" % t)
 
+    def newcols(t):
+        n = lambda s: s + str(t)
+        tt(A(n("wb"), 0, 64), A("nat", P, P + K), A(n("bk"), 0, 64), OP.subtract)
+        tt(A(n("wc"), 0, 64), A(n("wd"), 0, 64), A(n("wb"), 0, 64), OP.mult)
+        tt(A(n("we"), 0, 64), A(n("wc"), 0, 64), A(n("bk"), 0, 64), OP.add)
+
     def newlist(t):
         n = lambda s: s + str(t)
         gather("s", A(n("wg"), 0, 64), A(n("xm"), 0, 256), A(n("of"), 0, 4))
-        gather("s", A(n("wa"), 0, 64), A(n("M"), 0, 256), A(n("of"), 0, 4))
-        tt(A(n("wb"), 0, 64), A(n("wg"), 0, 64), A("nat", P, P + K), OP.mult)
-        ts(A(n("wd"), 0, 64), A(n("lk"), 0, 64), float(rank - 8), None, OP.is_equal)
-        tt(A(n("wc"), 0, 64), A(n("wb"), 0, 64), A(n("wa"), 0, 64), OP.subtract)
-        tt(A(n("we"), 0, 64), A(n("wd"), 0, 64), A(n("wc"), 0, 64), OP.mult)
-        tt(A(n("wf"), 0, 64), A(n("we"), 0, 64), A(n("wa"), 0, 64), OP.add)
+        tt(A(n("wf"), 0, 64), A(n("we"), 0, 64), A(n("wg"), 0, 64), OP.mult)
         scatter(A(n("M"), 0, 256), A(n("of"), 0, 4), A(n("wf"), 0, 64))
         m, mmx, c = n("M"), n("mm"), shift(t)
         scan(A(mmx, 0, P - c), A("sd", 0, P - c), A(m, c, P), OP.mult, OP.add)
@@ -510,29 +496,28 @@ def rank_program(g, core, T, topo):
 
     def finish(t):
         n = lambda s: s + str(t)
+        if t == 0:
+            if own == 0:
+                quant("W0", 0, 256, "tbt", 0)
+            act(A("ng", 1, 2), A("fb", 3, 4), AF.Copy, scale=-1.0)
+            lanes(0)
         if own == t:
             rebuild(t)
+        newcols(t)
         if t == 0:
             tt(A("M0", 0, P), A("xm0", 0, P), A("nat", 0, P), OP.mult)
+            act(A("sd", 0, 256), A("x16", 0, 256), AF.Sign)
         newlist(t)
         lists(t)
-        if t == 0:
-            const(A("D1", 0, 256), 0.0, A("nat", 0, 256))
-            if own:
-                owner()
-                owner_v()
+        if t == 0 and own:
+            owner()
+            owner_v()
+            owner_t()
         others = [o for o in range(NO) if 2 * o + t != rank]
         for s in ("", "s"):
             landed([A(n("W") + s, P + KO * o, P + KO * o + KO) for o in others], "new%d" % t + s, len(others) * full)
 
-    def after():
-        if own == 0:
-            owner()
-        act(A("ng", 1, 2), A("fb", 3, 4), AF.Copy, scale=-1.0)
-        lanes(0)
-        act(A("sd", 0, 256), A("x16", 0, 256), AF.Sign)
-
-    judge(0, "tA", after)
+    judge(0, "tA")
     finish(0)
     pick2("tB", 128, "W0", P + K, "ml0", 8)
     checks(1, "tB", lambda h: None, "s")
@@ -541,17 +526,21 @@ def rank_program(g, core, T, topo):
     quant("wq", 0, 128, "wt", 0)
     lanes(1)
     tt(A("M1", 0, P), A("xm1", 0, P), A("nat", 0, P), OP.mult)
-    judge(1, "tB", lambda: None)
+    judge(1, "tB")
     finish(1)
-    pick2("F", 128, "W1", P + K, "ml1", 8)
     for h in range(2):
-        mm(A("py", 512 * h, 512 * h + 128), "wq", 0, "F", 128 * h, 128 * h + 128)
+        mm(A("py", 512 * h, 512 * h + 128), "wq", 0, "W1", 128 * h, 128 * h + 128)
+        cp("s", A("ya", 128 * h, 128 * h + 128), A("py", 512 * h, 512 * h + 128))
+    pick2("F", 128, "W1", P + K, "ml1", 8)
+    mm(A("pc", 0, 128), "wq", 0, "W1", P + K - 128, P + K)
+    cp("v", A("ya", P, P + K), A("pc", 128 - K, 128))
+    for h, e in ((0, "v"), (1, "s")):
+        gather(e, A("yb", 128 * h, 128 * h + 128), A("ya", 0, P + K), A("ml1", 8 * h, 8 * h + 8))
+    for h in range(2):
         dma("y", None, A("F", 128 * h, 128 * h + 128), "st_c", 32, out_ap=T.oc[:, 512 * h:512 * h + 512],
             in_ap=T.F[:, 128 * h:128 * h + 128].bitcast(dt.uint8))
     for k in range(4):
         dma("y", None, A("Fs", 0, P, 1, 32 * k, 32 * k + 4), "st_s", 64, out_ap=T.osc[4 * k:4 * k + 4, :])
-    cp("v", A("yb", 0, 128), A("py", 0, 128))
-    cp("s", A("yb", 128, 256), A("py", 512, 640))
     dma("y", None, A("yb", 0, 128), "st_y", 32, out_ap=T.y[:, 0:128])
     dma("s", None, A("yb", 128, 256), "st_y", 32, out_ap=T.y[:, 128:256])
     for sem, val in final.items():

from concourse.bass import DstId, RemoteDMATransfer
from concourse.mybir import dt, AluOpType, AxisListType, ActivationFunctionType

OP = AluOpType
AF = ActivationFunctionType
X = AxisListType.X
N, P, K, NO, KO = 8, 256, 64, 4, 16
BIG = 1e29
STEP = 1.0 - 2.0 ** -24
TINY = 2.0 ** -118
FR = 2.0 ** -8

F4 = "float8_e4m3fn_x4"
SCRATCH = {}
VIEW = {}


def _sb(name, n, ty="float32"):
    SCRATCH[name] = ("sbuf", [128, n], ty)


def _mx(name, n):
    _sb(name, n, F4)
    _sb(name + "s", n, "uint8")


def _parts(buf, *parts):
    c = 0
    for name, n in parts:
        VIEW[name] = (buf, c)
        c += n + -n % 4
    _sb(buf, c)


for _n, _w in (("tbt", 4 * P), ("ut", 512), ("wt", 512), ("ee", 528), ("zt", 512)):
    _sb(_n, _w, "bfloat16")
_parts("con", ("rc", 40), ("hm", 32), ("jc", 1), ("hx", 32), ("hy", 32), ("rf", 40), ("dl0", 8), ("fb", 8), ("st", 2), ("sd32", 32),
       ("sp", 16), ("one", 32), ("frc", 32), ("oc", 8), ("klc", 16), ("ng", 4), ("eq0", 32), ("eq1", 32), ("dm0", 32), ("dm1", 32),
       ("gm0", 16), ("gm1", 16), ("lof", 4), ("vj0", 32), ("vj1", 32), ("pr", 64), ("l16", 64), ("t3", 64), ("t4", 64), ("t5", 64),
       ("t6", 64), ("t7", 64), ("t8", 64))
for _n, _w in (("nat", 528), ("x16", 272), ("xa0", 256), ("xa1", 256), ("xm0", 256), ("xm1", 256), ("md", 128),
               ("sd", 256), ("dpat", 128), ("yb", 256), ("ya", P + K), ("lt", 64), ("wt01", 64), ("tab", 128)):
    _sb(_n, _w)
_sb("pi", 2, "int32")
_sb("ib", 8, "int32")
_sb("cl", 2, "uint16")
_sb("lo", 4, "uint16")
_sb("dl", 8, "uint16")
_sb("gl", 2, "uint16")
for _n, _w in (("tA", P), ("tB", P), ("F", P), ("uq", 128), ("wq", 128), ("eq", 512)):
    _mx(_n, _w)
for _t in "01":
    _parts("jd" + _t, ("d1" + _t, 32), ("so" + _t, 32), ("du" + _t, 64), ("lw" + _t, 32), ("px" + _t, 16), ("tl" + _t, 64), ("rk" + _t, 4),
           ("tt" + _t, 128), ("xs" + _t, 8), ("ys" + _t, 8), ("xb" + _t, 4), ("jf" + _t, 4), ("fr" + _t, 4), ("zz" + _t, 16),
           ("zo" + _t, 8), ("nd" + _t, 1), ("wg" + _t, 64), ("wb" + _t, 64), ("wc" + _t, 64), ("wd" + _t, 64), ("we" + _t, 64),
           ("wf" + _t, 64), ("th" + _t, 256), ("cm" + _t, 260), ("ca" + _t, 2), ("cb" + _t, 2), ("ls" + _t, 2), ("rl" + _t, 256),
           ("cj" + _t, 256), ("lj" + _t, 16), ("mm" + _t, 256))
    for _n, _w in (("L", 32), ("S", 256), ("Lz", 64), ("val", 32), ("D", 256), ("dd", 128), ("bk", 64), ("lk", 64), ("M", 256)):
        _sb(_n + _t, _w)
    for _n, _w in (("R", 2), ("of", 4), ("cd", 4), ("oo", 2), ("lc", 2), ("ml", 16), ("oi", 8)):
        _sb(_n + _t, _w, "uint16")
    _sb("h" + _t, 512, "bfloat16")
    for _n, _w in (("slot", K), ("land", 256), ("ord", 128), ("new", 128), ("W", P + K)):
        _mx(_n + _t, _w)
SCRATCH["pc"] = ("psum", [128, 1024], "float32")
SCRATCH["dec"] = ("psum", [128, 2048], "float32")
SCRATCH["py"] = ("psum", [128, 1024], "float32")
PSUM = ("pc", "dec", "py")

SEMAPHORES = ["qv", "qs", "qt", "qg", "out", "ld_u", "ld_a", "ld_b", "ld_w", "st_c", "st_s", "st_y",
              "st_b0", "st_b1", "ck0", "ck1", "col0", "col0s", "col1", "col1s", "new0", "new0s", "new1", "new1s"]


def rank_program(g, core, T, topo):
    rank = T.rank_of(core)
    if rank is None:
        return
    eng = {"v": g.vector, "s": g.scalar, "t": g.tensor, "g": g, "y": g.sync}
    count = {"v": 0, "s": 0, "t": 0, "g": 0}
    seen = {e: {} for e in eng}
    wrote, read = {}, {}
    final = {}

    def A(name, c0, c1, st=1, p0=0, p1=128):
        if name in VIEW:
            name, c = VIEW[name]
            c0, c1 = c0 + c, c1 + c
        ap = T[name][p0:p1, c0:c1] if st == 1 else T[name][p0:p1, c0:c1:st]
        cols = frozenset(c // 512 for c in range(c0, c1, st)) if name in PSUM else frozenset(range(c0, c1, st))
        return (name, p0, p1, cols, ap)

    def hits(table, r):
        for (p0, p1, cols, tok) in table.get(r[0], ()):
            if p0 < r[2] and r[1] < p1 and not cols.isdisjoint(r[3]):
                yield tok

    def wait(e, sem, val):
        if seen[e].get(sem, 0) < val:
            eng[e].wait_ge(T.sem[sem], val)
            seen[e][sem] = val

    def order(e, ins, outs):
        need = {}
        for rs, table, same in ((ins, wrote, True), (outs, wrote, True), (outs, read, False)):
            for r in rs:
                for sem, val, src in hits(table, r):
                    if src != e or (same and r[0] not in PSUM) or rs is ins:
                        need[sem] = max(need.get(sem, 0), val)
        for sem, val in need.items():
            wait(e, sem, val)

    def note(ins, outs, tok):
        for r in ins:
            read.setdefault(r[0], []).append((r[1], r[2], r[3], tok))
        for r in outs:
            wrote.setdefault(r[0], []).append((r[1], r[2], r[3], tok))

    def op(e, outs, ins, call):
        order(e, ins, outs)
        inst = call()
        count[e] += 1
        inst.then_inc(T.sem["q" + e], 1)
        final["q" + e] = count[e]
        note(ins, outs, ("q" + e, count[e], e))

    def dma(e, out, in_, sem, total, out_ap=None, in_ap=None):
        order(e, [in_] if in_ else [], [out] if out else [])
        o = out_ap if out_ap is not None else out[4]
        i = in_ap if in_ap is not None else in_[4]
        eng[e].dma_start(o, i).then_inc(T.sem[sem], 16)
        final[sem] = total
        note([in_] if in_ else [], [out] if out else [], (sem, total, "dma"))

    def tt(out, a, b, o):
        op("v", [out], [a, b], lambda: g.vector.tensor_tensor(out[4], a[4], b[4], o))

    def ts(out, a, s1, s2, o0, o1=None):
        ins = [a] + [s for s in (s1, s2) if isinstance(s, tuple)]
        v1 = s1[4] if isinstance(s1, tuple) else s1
        v2 = s2[4] if isinstance(s2, tuple) else s2
        if o1 is None:
            op("v", [out], ins, lambda: g.vector.tensor_scalar(out[4], a[4], v1, None, o0))
        else:
            op("v", [out], ins, lambda: g.vector.tensor_scalar(out[4], a[4], v1, v2, o0, o1))

    def act(out, a, f, bias=None, scale=None, total=None):
        ins = [a] + [s for s in (bias, scale) if isinstance(s, tuple)]
        kw = {}
        if bias is not None:
            kw["bias"] = bias[4] if isinstance(bias, tuple) else bias
        if scale is not None:
            kw["scale"] = scale[4] if isinstance(scale, tuple) else scale
        if total is not None:
            kw["accum_out"] = total[4]
        op("s", [out] if total is None else [out, total], ins, lambda: g.scalar.activation(out[4], a[4], f, **kw))

    def cp(e, out, a):
        if e == "v":
            op("v", [out], [a], lambda: g.vector.tensor_copy(out[4], a[4]))
        else:
            act(out, a, AF.Copy)

    def fill(out, x):
        op("v", [out], [], lambda: g.vector.memset(out[4], x))

    def const(out, x, like):
        act(out, like, AF.Identity, bias=x, scale=0.0)

    def red(out, a, o):
        op("v", [out], [a], lambda: g.vector.tensor_reduce(out[4], a[4], X, o))

    def scan(out, d0, d1, o0, o1, first=None):
        op("v", [out], [d0, d1] + ([first] if first else []),
           lambda: g.vector.tensor_tensor_scan(out[4], d0[4], d1[4], first[4] if first else 0.0, o0, o1))

    def turn(out, a):
        op("v", [out], [a], lambda: g.vector.transpose(out[4], a[4]))

    def iota(out, pat, base, cm, flag=True):
        kw = {"allow_small_or_imprecise_dtypes": True} if flag else {}
        op("g", [out], [], lambda: g.iota(out[4], pat, base, cm, **kw))

    def gather(e, out, win, off, f=AF.Copy):
        if e == "v":
            op("v", [out], [win, off], lambda: g.vector.tensor_copy(out[4], win[4].indirect(off[4])))
        else:
            op("s", [out], [win, off], lambda: g.scalar.activation(out[4], win[4].indirect(off[4]), f))

    def gather_tt(out, win, off, b, o):
        op("v", [out], [win, off, b], lambda: g.vector.tensor_tensor(out[4], win[4].indirect(off[4]), b[4], o))

    def scatter(win, off, val):
        op("v", [win], [val, off], lambda: g.vector.tensor_copy(win[4].indirect(off[4]), val[4]))

    def pickc(dst, c0, c1, src, n, off):
        o, i = A(dst, c0, c1), A(src, 0, n)
        op("v", [o], [i, off], lambda: g.vector.tensor_copy(o[4].bitcast(dt.uint32), i[4].bitcast(dt.uint32).indirect(off[4])))

    def picks(e, dst, c0, c1, src, n, off):
        gather(e, A(dst + "s", c0, c1), A(src + "s", 0, n), off)

    def pick(dst, c0, c1, src, n, off):
        pickc(dst, c0, c1, src, n, off)
        picks("s", dst, c0, c1, src, n, off)

    def pick2(dst, n1, src, n, off, k):
        for h in range(2):
            pickc(dst, n1 * h, n1 * h + n1, src, n, A(off, k * h, k * h + k))
        for h, e in ((0, "s"), (1, "v")):
            picks(e, dst, n1 * h, n1 * h + n1, src, n, A(off, k * h, k * h + k))

    def quant(dst, c0, c1, tile, at):
        o, s, i = A(dst, c0, c1), A(dst + "s", c0, c1), A(tile, at, at + 4 * (c1 - c0))
        op("v", [o, s], [i], lambda: g.vector.quantize_mx(o[4], s[4], i[4]))

    def mm(out, lhs, a, rhs, b0, b1):
        l, ls, r, rs = A(lhs, a, a + 128), A(lhs + "s", a, a + 128), A(rhs, b0, b1), A(rhs + "s", b0, b1)
        op("t", [out], [l, ls, r, rs], lambda: g.tensor.matmul_mx(out[4], l[4], ls[4], r[4], rs[4], True, True))

    peers = [c for c in T.cores if c != core]

    def dest(c):
        rid, pid, _s = topo.addr(c)
        return DstId(rid=rid, pnc=pid)

    def raw(r, codes):
        return r[4].bitcast(dt.uint8) if codes else r[4]

    def spread(ref, sem, codes=False):
        order("g", [ref], [])
        m = topo.mask(core, peers[0])
        for c in peers:
            m &= topo.mask(core, c)
        g.remote_dma_fused([RemoteDMATransfer(dst_ids=[dest(c) for c in peers], dma_engine_mask=m, remote_sem=T.sem[sem],
                                              srcs=[raw(ref, codes)], dsts=[raw(ref, codes) for _ in peers])],
                           local_sem=T.sem["out"])
        final["out"] = final.get("out", 0) + bin(m).count("1")

    full = len(topo.engines(core, peers[0]))

    def landed(refs, sem, total):
        note([], refs, (sem, total, "remote"))
        final[sem] = total

    def deal(t, codes):
        tr = []
        for o in range(NO):
            c = T.cores[2 * o + t]
            if c == core:
                continue
            es = topo.engines(core, c)
            w = len(es) // NO
            s = "" if codes else "s"
            src = A("slot%d" % t + s, KO * o, KO * o + KO)
            order("g", [src], [])
            d = A("land%d" % t + s, KO * rank, KO * rank + KO)
            tr.append(RemoteDMATransfer(dst_ids=[dest(c)], dma_engine_mask=sum(1 << e for e in es[w * o:w * o + w]),
                                        remote_sem=T.sem["col%d" % t + s], srcs=[raw(src, codes)], dsts=[raw(d, codes)]))
            final["out"] = final.get("out", 0) + w
        g.remote_dma_fused(tr, local_sem=T.sem["out"])

    own = rank % 2
    o_ = rank // 2
    a0 = KO * o_

    dma("y", A("tbt", 0, 512), None, "ld_a", 16, in_ap=T.tb[:, 0:512])
    dma("s", A("ut", 0, 8), None, "ld_u", 16, in_ap=T.u[:, 0:8])
    dma("s", A("tbt", 512, 1024), None, "ld_b", 16, in_ap=T.tb[:, 512:1024])
    wait("y", "ld_b", 16)
    dma("y", A("wt", 0, 512), None, "ld_w", 16, in_ap=T.w[:])

    iota(A("pi", 0, 2), [[1, 2]], 0, 1, False)
    iota(A("nat", 0, 128), [[1, 128]], 0, 0)
    iota(A("rc", 0, 40), [[0, 5], [1, 8]], 0, 0)
    iota(A("hm", 0, 32), [[0, 2], [1, 2], [0, 8]], 0, 0)
    iota(A("jc", 0, 1), [[1, 1]], 0, 1)
    iota(A("lt", 0, 64), [[0, 8], [1, 8]], 0, 0)
    iota(A("pr", 0, 64), [[16, 8], [0, 8]], 0, 0)
    iota(A("hx", 0, 32), [[128, 2], [1, 16]], 0, 0)
    iota(A("dl0", 0, 8), [[16, 4], [0, 2]], 0, 0)
    fill(A("ut", 8, 512), 0.0)
    fill(A("one", 0, 32), 1.0)
    fill(A("frc", 0, 32), FR)
    for col, (src, bits) in enumerate(((0, 7), (1, 7), (0, 31), (0, 15), (0, 8), (0, 112), (0, 64), (0, 32))):
        ts(A("ib", col, col + 1), A("pi", src, src + 1), bits, None, OP.bitwise_and)
    cp("v", A("fb", 0, 8), A("ib", 0, 8))

    def masks(t):
        n = str(t)
        ts(A("eq" + n, 0, 32), A("rc", 0, 32), A("fb", t, t + 1), -1.0, OP.is_equal, OP.mult)
        ts(A("gm" + n, 0, 16), A("rc", 0, 16), A("fb", t, t + 1), BIG, OP.is_equal, OP.mult)
        tt(A("dm" + n, 0, 32), A("eq" + n, 0, 32), A("hm", 0, 32), OP.add)

    masks(0)
    quant("uq", 0, 128, "ut", 0)
    act(A("nat", 128, 256), A("nat", 0, 128), AF.Identity, bias=128.0)
    act(A("nat", 256, 512), A("nat", 0, 256), AF.Identity, bias=256.0)
    act(A("nat", 512, 528), A("nat", 0, 16), AF.Identity, bias=512.0)
    act(A("ng", 0, 1), A("jc", 0, 1), AF.Identity, bias=4.0, scale=4.0)

    def checks(t, tab, half, e0):
        for h in range(2):
            half(h)
            mm(A("pc", 512 * h, 512 * h + 128), tab, 128 * h, "uq", 0, 128)
        for h, e in ((0, e0), (1, "v")):
            cp(e, A("L%d" % t, 4 * rank + 2 * h, 4 * rank + 2 * h + 2), A("pc", 512 * h, 512 * h + 2))
        spread(A("L%d" % t, 4 * rank, 4 * rank + 4), "ck%d" % t)
        landed([A("L%d" % t, 4 * r, 4 * r + 4) for r in range(N) if r != rank], "ck%d" % t, 7 * full)

    checks(0, "tA", lambda h: quant("tA", 128 * h, 128 * h + 128, "tbt", 512 * h), "v")

    iota(A("D0", 0, 256), [[0, 256]], 0, 0)
    iota(A("x16", 0, 272), [[0, 17], [1, 16]], 0, 0)
    iota(A("D1", 0, 256), [[0, 256]], 0, 0)
    ts(A("lo", 0, 1), A("fb", 0, 1), 4.0, None, OP.mult)
    ts(A("lo", 1, 2), A("fb", 0, 1), 4.0, 2.0, OP.mult, OP.add)
    act(A("lof", 0, 1), A("fb", 4, 5), AF.Identity, bias=1.0, scale=0.25)
    act(A("lof", 1, 2), A("fb", 0, 1), AF.Identity, bias=A("lof", 0, 1), scale=4.0)
    cp("s", A("sd32", 0, 32), A("one", 0, 32))
    const(A("sd32", 0, 32, 16), 0.0, A("nat", 0, 2))
    const(A("sp", 0, 16), 0.0, A("nat", 0, 16))
    const(A("sp", 0, 16, 8), -BIG, A("nat", 0, 2))
    act(A("rf", 0, 40), A("rc", 0, 40), AF.Copy, scale=8.0 * FR)
    for t in "01":
        const(A("cm" + t, 256, 257), 128.0, A("nat", 0, 1))

    def owner():
        act(A("oc", 0, 1), A("fb", 0, 1), AF.Identity, bias=-16.0, scale=16.0)
        act(A("oc", 1, 2), A("fb", 0, 1), AF.Relu, bias=-16.0, scale=16.0)
        act(A("oc", 2, 3), A("fb", 0, 1), AF.Relu, bias=1.0, scale=-1.0)
        act(A("oc", 3, 4), A("fb", 4, 5), AF.Copy, scale=0.125)
        act(A("oc", 4, 5), A("fb", 4, 5), AF.Identity, bias=1.0, scale=-0.125)
        act(A("oc", 5, 6), A("fb", 4, 5), AF.Copy, scale=8.0)
        act(A("oc", 6, 7), A("fb", 4, 5), AF.Identity, bias=7.0)
        act(A("klc", 0, 8), A("nat", 0, 8), AF.Copy, scale=A("oc", 4, 5))
        act(A("klc", 8, 16), A("nat", 8, 16), AF.Copy, scale=A("oc", 3, 4))
        act(A("l16", 0, 64), A("lt", 0, 64), AF.Copy, scale=16.0)
        act(A("t4", 0, 64), A("pr", 0, 64), AF.Identity, bias=A("oc", 1, 2), scale=A("oc", 2, 3))
        const(A("dpat", 0, 128), 1.0, A("nat", 0, 128))
        const(A("dpat", 0, 128, 8), 0.0, A("nat", 0, 16))
        const(A("dpat", 1, 128, 8), -1.0, A("nat", 0, 16))

    def owner_v():
        fill(A("zt", 0, 512), 0.0)
        ts(A("ee", 0, 528), A("nat", 0, 528), A("ng", 0, 1), None, OP.is_equal)
        quant("land%d" % own, 128, 256, "zt", 0)
        for b in range(4):
            quant("eq", 128 * b, 128 * b + 128, "ee", 4 - b)
        ts(A("cl", 0, 1), A("fb", 0, 1), 16.0, A("oc", 6, 7), OP.mult, OP.add)

    def owner_t():
        ts(A("t3", 0, 64), A("pr", 0, 64), A("oc", 0, 1), 16.0, OP.is_le, OP.mult)
        tt(A("t5", 0, 64), A("t3", 0, 64), A("t4", 0, 64), OP.add)
        tt(A("t6", 0, 64), A("t5", 0, 64), A("l16", 0, 64), OP.is_equal)
        act(A("t7", 0, 64), A("t6", 0, 64), AF.Copy, scale=128.0)
        tt(A("t8", 0, 64), A("t5", 0, 64), A("t7", 0, 64), OP.add)
        act(A("tab", 0, 64), A("t8", 0, 64), AF.Copy, scale=A("oc", 4, 5))
        act(A("tab", 64, 128), A("t8", 0, 64), AF.Copy, scale=A("oc", 3, 4))

    cp("v", A("lo", 2, 3), A("lof", 1, 2))
    ts(A("gl", 0, 1), A("fb", 2, 3), 0.0, None, OP.add)
    ts(A("gl", 1, 2), A("fb", 2, 3), 32.0, None, OP.add)
    if own == 0:
        owner()
        owner_v()
    else:
        quant("W0", 0, 256, "tbt", 0)
    act(A("st", 0, 1), A("fb", 6, 7), AF.Identity, bias=1.0, scale=(STEP - 1.0) / 64)
    act(A("st", 1, 2), A("fb", 7, 8), AF.Identity, bias=1.0, scale=(STEP - 1.0) / 32)
    for s, c in ((1, 0), (2, 1), (3, 0)):
        act(A("md", 32 * s, 32 * s + 32), A("one", 0, 32), AF.Copy, scale=A("st", c, c + 1))
    ts(A("md", 0, 32), A("nat", 0, 32), A("fb", 2, 3), STEP, OP.is_ge, OP.max)
    ts(A("dl", 0, 8), A("dl0", 0, 8), A("fb", 3, 4), None, OP.add)
    ts(A("hy", 0, 32), A("hx", 0, 32), A("fb", 5, 6), None, OP.add)
    for t in range(2):
        tt(A("vj%d" % t, 0, 32), A("hy", 0, 32), A("rf", t, t + 32), OP.add)
    if own == 0:
        owner_t()
    ts(A("wt01", 0, 64), A("lt", 0, 64), float(rank), None, OP.is_equal)

    def shift(t):
        return rank if t == 0 else -rank % P

    def lanes(t):
        n, c = str(t), -shift(t) % 16
        act(A("xa" + n, 0, 256), A("x16", c, c + 256), AF.Abs, bias=A("ng", 1, 2))
        act(A("xm" + n, 0, 256), A("xa" + n, 0, 256), AF.Relu, bias=1.0, scale=-1.0)

    def judge(t, tab):
        n = lambda s: s + str(t)
        L, d1, so, du, S, lw, px, tl = n("L"), n("d1"), n("so"), n("du"), n("S"), n("lw"), n("px"), n("tl")
        th, cm, cj, rl, ca, cb, ls, rk, R = n("th"), n("cm"), n("cj"), n("rl"), n("ca"), n("cb"), n("ls"), n("rk"), n("R")
        i = A(L, 0, 32)
        gather_tt(A(d1, 0, 32), i, A("lo", 0, 2), A(n("dm"), 0, 32), OP.mult)
        gather("s", A(lw, 0, 16), i, A("lo", 2, 3), AF.Abs)
        scan(A(so, 0, 32), A("sd32", 0, 32), A(d1, 0, 32), OP.mult, OP.subtract)
        for h in range(2):
            act(A(du, 32 * h, 32 * h + 32), A("one", 0, 32), AF.Abs, bias=TINY, scale=A(so, 16 * h + 15, 16 * h + 16))
        tt(A(lw, 16, 32), A(lw, 0, 16), A(n("gm"), 0, 16), OP.subtract)
        scan(A(px, 0, 16), A("sp", 0, 16), A(lw, 16, 32), OP.add, OP.max)
        for h in range(2):
            turn(A(S, 128 * h, 128 * h + 32), A(du, 32 * h, 32 * h + 32))
        for h in range(2):
            act(A(n("lj"), 8 * h, 8 * h + 8), A(px, 8 * h, 8 * h + 8), AF.Sign, bias=A(px, 8 * h + 7, 8 * h + 8), scale=-1.0,
                total=A(ls, h, h + 1))
        for h in range(2):
            act(A(tl, 32 * h, 32 * h + 32), A("frc", 0, 32), AF.Copy, scale=A(ls, h, h + 1))
        for h in (0, 128):
            cp("v", A(S, h + 32, h + 64, 1, 0, 64), A(S, h, h + 32, 1, 64, 128))
            cp("s", A(S, h + 32, h + 64, 1, 64, 128), A(S, h, h + 32, 1, 0, 64))
        ts(A(th, 128, 256), A("md", 0, 128), A(du, 32, 33), None, OP.mult)
        for h in (0, 128):
            for a, e in ((0, "v"), (2, "s"), (1, "v"), (3, "s")):
                b = a ^ 1
                cp(e, A(S, h + 64, h + 128, 1, 32 * a, 32 * a + 32), A(S, h, h + 64, 1, 32 * b, 32 * b + 32))
        turn(A(n("Lz"), 0, 64), A(tl, 0, 64))
        gather_tt(A(n("val"), 0, 32), A(n("Lz"), 0, 64), A("gl", 0, 2), A("vj%d" % t, 0, 32), OP.add)
        act(A(th, 0, 128), A("md", 0, 128), AF.Copy, scale=A(du, 0, 1))
        act(A(n("nd"), 0, 1), A(du, 0, 1), AF.Copy, scale=-1.0)
        act(A(rl, 128, 256), A(S, 0, 128), AF.Relu, bias=A(du, 32, 33), scale=-1.0)
        act(A(rl, 0, 128), A(S, 128, 256), AF.Relu, bias=A(n("nd"), 0, 1))
        act(A(cj, 128, 256), A(rl, 128, 256), AF.Sign, scale=-1.0, total=A(ca, 1, 2))
        act(A(cj, 0, 128), A(rl, 0, 128), AF.Sign, total=A(ca, 0, 1))
        for h in (1, 0):
            tt(A(cm, 128 * h, 128 * h + 128), A(S, 128 * h, 128 * h + 128), A(th, 128 * h, 128 * h + 128), OP.is_gt)
        red(A(cb, 1, 2), A(cm, 128, 257), OP.add)
        red(A(cb, 0, 1), A(cm, 0, 128), OP.add)
        tt(A(rk, 0, 2), A(ca, 0, 2), A(cb, 0, 2), OP.add)
        cp("v", A(R, 0, 2), A(rk, 0, 2))
        scatter(A(n("D"), 0, 256), A(R, 0, 2), A(n("val"), 0, 32))
        gather("v", A(n("dd"), 0, 128), A(n("D"), 0, 64), A("dl", 0, 8))
        turn(A(n("tt"), 0, 128), A(n("dd"), 0, 128))
        xs, ys, xb, of = n("xs"), n("ys"), n("xb"), n("of")
        tt(A(xs, 0, 4), A(n("tt"), 0, 128, 32), A(n("tt"), 16, 128, 32), OP.add)
        cp("v", A(xs, 4, 8, 1, 0, 64), A(xs, 0, 4, 1, 64, 128))
        cp("s", A(xs, 4, 8, 1, 64, 128), A(xs, 0, 4, 1, 0, 64))
        tt(A(ys, 0, 4), A(xs, 0, 4), A(xs, 4, 8), OP.add)
        for a, e in ((0, "v"), (2, "s"), (1, "v"), (3, "s")):
            b = a ^ 1
            cp(e, A(ys, 4, 8, 1, 32 * a, 32 * a + 32), A(ys, 0, 4, 1, 32 * b, 32 * b + 32))
        tt(A(xb, 0, 4), A(ys, 0, 4), A(ys, 4, 8), OP.add)
        cp("v", A(of, 0, 4), A(xb, 0, 4))
        pick(n("slot"), 0, K, tab, P, A(of, 0, 4))
        deal(t, True)
        deal(t, False)
        cp("v", A(n("jf"), 0, 4), A(of, 0, 4))
        if own == t:
            cp("v", A(n("oo"), 0, 1), A(xb, o_, o_ + 1))
            pick(n("land"), KO * rank, KO * rank + KO, tab, P, A(n("oo"), 0, 1))
        tt(A(n("fr"), 0, 4), A(xb, 0, 4), A(n("jf"), 0, 4), OP.subtract)
        if own == t:
            ts(A(n("lc"), 0, 1), A(n("fr"), o_, o_ + 1), 1.0 / FR, A("oc", 5, 6), OP.mult, OP.add)
            gather_tt(A(n("zz"), 0, 16), A("tab", 0, 128), A(n("lc"), 0, 1), A("klc", 0, 16), OP.add)
            tt(A(n("zo"), 0, 8), A(n("zz"), 0, 8), A(n("zz"), 8, 16), OP.add)
            cp("v", A(n("oi"), 0, 8), A(n("zo"), 0, 8))
        ts(A(n("cd"), 0, 4), A(n("fr"), 0, 4), 1.0 / FR, None, OP.mult)
        gather("s", A(n("bk"), 0, 64), A("nat", 0, 256), A(of, 0, 4))
        gather("s", A(n("wd"), 0, 64), A("wt01", 0, 64), A(n("cd"), 0, 4))

    def lists(t):
        n = lambda s: s + str(t)
        gather("s", A(n("lk"), 0, 64), A("lt", 0, 64), A(n("cd"), 0, 4))
        dma("y", None, A(n("bk"), 0, 64, 1, 0, 1), "st_b%d" % t, 32, out_ap=T.bs[2 * t:2 * t + 1, :])
        dma("y", None, A(n("lk"), 0, 64, 1, 0, 1), "st_b%d" % t, 32, out_ap=T.bs[2 * t + 1:2 * t + 2, :])

    def rebuild(t):
        n = lambda s: s + str(t)
        for s in ("", "s"):
            landed([A(n("land") + s, KO * r, KO * r + KO) for r in range(N) if r != rank], "col%d" % t + s, 7 * (full // NO))
        pick2(n("ord"), 64, n("land"), 256, n("oi"), 4)
        for b in range(4):
            mm(A("dec", 512 * b, 512 * b + 128), "eq", 128 * b, n("ord"), 0, 128)
        for b in range(4):
            scan(A(n("h"), b, 512, 4), A("dpat", 0, 128), A("dec", 512 * b, 512 * b + 128), OP.mult, OP.subtract)
        quant(n("new"), 0, 128, n("h"), 0)
        pick(n("W"), P + a0, P + a0 + KO, n("new"), 128, A("cl", 0, 1))
        spread(A(n("W"), P + a0, P + a0 + KO), "new%d" % t, True)
        spread(A(n("W") + "s", P + a0, P + a0 + KO), "new%ds" % t)

    def newcols(t):
        n = lambda s: s + str(t)
        tt(A(n("wb"), 0, 64), A("nat", P, P + K), A(n("bk"), 0, 64), OP.subtract)
        tt(A(n("wc"), 0, 64), A(n("wd"), 0, 64), A(n("wb"), 0, 64), OP.mult)
        tt(A(n("we"), 0, 64), A(n("wc"), 0, 64), A(n("bk"), 0, 64), OP.add)

    def newlist(t):
        n = lambda s: s + str(t)
        gather("s", A(n("wg"), 0, 64), A(n("xm"), 0, 256), A(n("of"), 0, 4))
        tt(A(n("wf"), 0, 64), A(n("we"), 0, 64), A(n("wg"), 0, 64), OP.mult)
        scatter(A(n("M"), 0, 256), A(n("of"), 0, 4), A(n("wf"), 0, 64))
        m, mmx, c = n("M"), n("mm"), shift(t)
        scan(A(mmx, 0, P - c), A("sd", 0, P - c), A(m, c, P), OP.mult, OP.add)
        if c:
            scan(A(mmx, P - c, P), A("sd", P - c, P), A(m, 0, c), OP.mult, OP.add, A(mmx, P - c - 1, P - c))
        cp("v", A(n("ml"), 0, 16), A(mmx, 15, 256, 16))

    def finish(t):
        n = lambda s: s + str(t)
        if t == 0:
            if own == 0:
                quant("W0", 0, 256, "tbt", 0)
            act(A("ng", 1, 2), A("fb", 3, 4), AF.Copy, scale=-1.0)
            lanes(0)
        if own == t:
            rebuild(t)
        newcols(t)
        if t == 0:
            tt(A("M0", 0, P), A("xm0", 0, P), A("nat", 0, P), OP.mult)
            act(A("sd", 0, 256), A("x16", 0, 256), AF.Sign)
        newlist(t)
        lists(t)
        if t == 0 and own:
            owner()
            owner_v()
            owner_t()
        others = [o for o in range(NO) if 2 * o + t != rank]
        for s in ("", "s"):
            landed([A(n("W") + s, P + KO * o, P + KO * o + KO) for o in others], "new%d" % t + s, len(others) * full)

    judge(0, "tA")
    finish(0)
    pick2("tB", 128, "W0", P + K, "ml0", 8)
    checks(1, "tB", lambda h: None, "s")
    pick("W1", 0, P, "W0", P + K, A("ml0", 0, 16))
    masks(1)
    quant("wq", 0, 128, "wt", 0)
    lanes(1)
    tt(A("M1", 0, P), A("xm1", 0, P), A("nat", 0, P), OP.mult)
    judge(1, "tB")
    finish(1)
    for h in range(2):
        mm(A("py", 512 * h, 512 * h + 128), "wq", 0, "W1", 128 * h, 128 * h + 128)
        cp("s", A("ya", 128 * h, 128 * h + 128), A("py", 512 * h, 512 * h + 128))
    pick2("F", 128, "W1", P + K, "ml1", 8)
    mm(A("pc", 0, 128), "wq", 0, "W1", P + K - 128, P + K)
    cp("v", A("ya", P, P + K), A("pc", 128 - K, 128))
    for h, e in ((0, "v"), (1, "s")):
        gather(e, A("yb", 128 * h, 128 * h + 128), A("ya", 0, P + K), A("ml1", 8 * h, 8 * h + 8))
    for h in range(2):
        dma("y", None, A("F", 128 * h, 128 * h + 128), "st_c", 32, out_ap=T.oc[:, 512 * h:512 * h + 512],
            in_ap=T.F[:, 128 * h:128 * h + 128].bitcast(dt.uint8))
    for k in range(4):
        dma("y", None, A("Fs", 0, P, 1, 32 * k, 32 * k + 4), "st_s", 64, out_ap=T.osc[4 * k:4 * k + 4, :])
    dma("y", None, A("yb", 0, 128), "st_y", 32, out_ap=T.y[:, 0:128])
    dma("s", None, A("yb", 128, 256), "st_y", 32, out_ap=T.y[:, 128:256])
    for sem, val in final.items():
        wait("g", sem, val)
